import numpy as np, ml_dtypes
CORES = [1,5,17,21,33,37,49,53]
N = 8
BF = ml_dtypes.bfloat16
def gentries(a):
    return np.ascontiguousarray(a.reshape(8, 16, -1).transpose(0, 2, 1)).reshape(8, -1)
def gtable(e):
    e = np.asarray(e); return np.ascontiguousarray(e.reshape(8, -1, 16).transpose(0, 2, 1)).reshape(128, -1).astype(np.int32)
V, D, M, R = 1024, 8, 32, 2
def joined(x):
    return np.stack([gentries(x[r]).reshape(8, D, V) for r in range(N)], 2).reshape(8, D, N * V)
def pack(p, a, w):
    pin, inc = [np.stack([gtable(x.reshape(8, D, N, V)[:, :, r].reshape(8, D * V)) for r in range(N)]) for x in (p, np.argsort(p, -1))]
    return {"part": np.ascontiguousarray(a.transpose(1, 0, 2)).astype(np.int32), "pin": pin, "inc": inc, "w": np.ascontiguousarray(w).astype(np.int32)}
def mix(rng, p, share):
    p = np.array(p); s = np.flatnonzero(rng.random(p.size) < share); p[s] = rng.permutation(p[s]); return p
def clusters(rng, noise):
    p = np.zeros((8, D, N * V), np.int64); h = rng.integers(0, 16, (8, N * V))
    for g in range(8):
        e = np.argsort(rng.permutation(h[g]), kind="stable")
        for i in range(D):
            p[g, i, e] = np.lexsort((rng.random(N * V), h[g])); p[g, i] = mix(rng, p[g, i], noise[g])
    return p, h
def spoil(rng, h, share):
    return np.where(rng.random((8, N, V)) < share, rng.integers(0, 16, (8, N, V)), h.reshape(8, N, V))
def setup_inputs(rng):
    p, h = clusters(rng, rng.random(8) * 0.15)
    return pack(p, spoil(rng, h, rng.random((8, N, 1)) * 0.3), rng.integers(0, 16, (N, 8, V)))
def setup_inputs_ties(rng):
    p = np.stack([np.stack([rng.permutation(N * V) for i in range(D)]) for g in range(8)])
    w = rng.integers(1, 16, (1, 8, 1)) * np.where(np.arange(8)[None, :, None] & 1, rng.integers(0, 2, (N, 8, V)), 1)
    return pack(p, rng.integers(0, 16, (8, N, V)), w)
def setup_inputs_cap(rng):
    n = rng.random(8) * 0.15; n[:3] = 0; p, h = clusters(rng, n); a = spoil(rng, h, rng.random((8, N, 1)) * 0.3)
    w = rng.integers(0, 16, (N, 8, V)); w[:, :3] = np.maximum(w[:, :3], 1); inv = np.argsort(p, -1)
    for g in range(3):
        m = np.array(h[g]); busy = np.zeros(N * V, bool); want = np.roll(np.array([M, M + 1, M - 1, 0, M, 1, M + 1, M // 2])[:N], g)
        for r in range(N):
            left = int(want[r])
            for v in rng.permutation(V // 2) * 2 + (r * V + (g == 2)):
                if left == 0: break
                e = inv[g, :, v]
                if busy[e].any() or len(set(e.tolist())) < D: continue
                busy[e] = True; m[v] = (h[g, v] + rng.integers(1, 16)) & 15; left -= 1
        a[g] = m.reshape(N, V)
    return pack(p, a, w)
def setup_inputs_twins(rng):
    p = np.zeros((8, D, N * V), np.int64); j = np.arange(N * V); a = np.zeros((8, N, V), np.int64)
    for g in range(8):
        b = j if g == 0 else (j + V) % (N * V) if g == 1 else rng.permutation(N * V); s = 0.3 + 0.5 * rng.random()
        for i in range(D): p[g, i] = b if i == 0 else mix(rng, b, s)
        u = rng.permutation(16)[:rng.integers(2, 17)]; a[g] = u[rng.integers(0, u.size, (N, V))]
    return pack(p, a, rng.integers(0, 16, (N, 8, V)))
def setup_inputs_spread(rng):
    p, h = clusters(rng, rng.random(8)); k = 2.0 ** rng.integers(0, 5, (8, N, 1))
    q = np.minimum((16 * rng.random((8, N, V)) ** k).astype(np.int64), 15)
    a = np.where(rng.random((8, N, V)) < rng.random((8, N, 1)), q, h.reshape(8, N, V))
    w = np.where(rng.random((N, 8, V)) < rng.random((N, 8, 1)), rng.choice(np.array([0, 15]), (N, 8, V)), rng.integers(0, 16, (N, 8, V)))
    return pack(p, a, w)
def check_inputs(d):
    bad = [n for n, top in (("part", 16), ("pin", N * V), ("inc", N * V), ("w", 16)) if np.min(d[n]) < 0 or np.max(d[n]) >= top]
    if not bad:
        p, q, j = joined(d["pin"]), joined(d["inc"]), np.arange(N * V)
        if (np.sort(p, -1) != j).any(): bad.append("every vertex once at each position of pin")
        elif (np.take_along_axis(q, p, -1) != j).any(): bad.append("inc is the inverse of pin")
    return bad
def counts(a, p):
    return np.sum(a[p][None] == np.arange(16)[:, None, None], 1)
def reference(part, pin, inc, w):
    a = np.array(part.transpose(1, 0, 2)).reshape(8, N * V).astype(np.int64); wt = np.array(w.transpose(1, 0, 2)).reshape(8, N * V).astype(np.int64)
    p, e, j = joined(pin), joined(inc), np.arange(N * V); cut = np.zeros(8, np.int64)
    for g in range(8):
        for t in range(R):
            c = counts(a[g], p[g]); one = wt[g] * (c == 1); none = wt[g] * (c == 0)
            gain = np.sum(one[np.broadcast_to(a[g], (D, N * V)), e[g]], 0) - np.sum(none[:, e[g]], 1)
            gain[a[g], j] = -1000000
            best = np.argmax(gain, 0)
            can = ((gain[best, j] > 0) & (((j % V) + t) % 2 == 0)).reshape(N, V)
            go = (can & (np.add.accumulate(can.astype(np.int64), 1) <= M)).reshape(-1)
            a[g] = np.where(go, best, a[g])
        cut[g] = np.sum(wt[g] * (np.sum(counts(a[g], p[g]) > 0, 0) - 1))
    return {"newpart": np.ascontiguousarray(a.reshape(8, N, V).transpose(1, 0, 2)).astype(np.float32), "cut": np.repeat(cut.astype(np.float32)[None, :, None], N, 0)}

@@ -1,0 +1,428 @@
+from concourse.bass import DstId, RemoteDMATransfer
+from concourse.mybir import AluOpType, AxisListType, ActivationFunctionType
+
+PAD = 288
+NV = 8192
+DW = 32 + 2048
+ORDER = "xxakaaaxkaakaabababbabbbbabbababbb"
+
+SCRATCH = {
+    "SA": ("dram", [8, 128, 16], "int32"), "LA": ("dram", [8, 128, 16], "int32"),
+    "SP": ("dram", [8, 128, 64], "int32"), "LP": ("dram", [8, 128, 64], "int32"),
+    "SI": ("dram", [8, 128, 64], "int32"), "LI": ("dram", [8, 128, 64], "int32"),
+    "SN": ("dram", [8, 128, 8], "float32"), "LN": ("dram", [8, 128, 8], "float32"),
+    "SU": ("dram", [128, 2], "float32"), "LU": ("dram", [8, 128, 2], "float32"),
+    "win": ("sbuf", [128, NV], "bfloat16"), "G": ("sbuf", [128, PAD + NV], "bfloat16"),
+    "Z": ("sbuf", [128, NV], "bfloat16"), "Y": ("sbuf", [128, 4096], "bfloat16"),
+    "Di": ("sbuf", [128, DW], "int32"), "P": ("sbuf", [128, 1024], "float32"),
+    "pinI": ("sbuf", [128, 512], "int32"), "incI": ("sbuf", [128, 512], "int32"),
+    "pinU": ("sbuf", [128, 512], "uint16"), "incU": ("sbuf", [128, 512], "uint16"),
+    "Ai": ("sbuf", [128, 256], "int32"), "Wi": ("sbuf", [128, 256], "int32"),
+    "Ab": ("sbuf", [128, 256], "bfloat16"), "Wb": ("sbuf", [128, 256], "bfloat16"),
+    "junk": ("sbuf", [128, 256], "bfloat16"),
+    "Sel": ("sbuf", [128, 4096], "bfloat16"), "reset": ("sbuf", [128, 256], "float32"),
+    "kI": ("sbuf", [128, 8], "int32"), "kF": ("sbuf", [128, 32], "float32"),
+    "im": ("sbuf", [128, 128], "float32"), "iM": ("sbuf", [128, 128], "float32"), "pM": ("sbuf", [128, 128], "float32"),
+    "i32": ("sbuf", [128, 32], "float32"), "iK": ("sbuf", [128, 32], "float32"), "posc": ("sbuf", [128, 64], "float32"),
+    "posb": ("sbuf", [128, 64], "float32"),
+    "Idb": ("sbuf", [128, 128], "bfloat16"), "Id32": ("sbuf", [128, 32], "float32"), "TB": ("sbuf", [128, 128], "bfloat16"),
+    "t0": ("sbuf", [128, 128], "bfloat16"), "t1": ("sbuf", [128, 128], "bfloat16"),
+    "onesb": ("sbuf", [128, 128], "bfloat16"), "onesm": ("sbuf", [128, 128], "bfloat16"), "onesf": ("sbuf", [128, 8], "float32"),
+    "maskR": ("sbuf", [128, 128], "float32"), "Q8": ("sbuf", [128, 8], "float32"), "NE": ("sbuf", [128, 8], "float32"),
+    "SelS": ("sbuf", [128, 16], "bfloat16"), "LZ": ("sbuf", [128, 128], "bfloat16"),
+    "LC": ("sbuf", [128, 16], "bfloat16"), "LO": ("sbuf", [128, 16], "bfloat16"), "f": ("sbuf", [128, 256], "float32"),
+    "own": ("sbuf", [128, 64], "bfloat16"), "mins": ("sbuf", [128, 512], "float32"),
+    "ki": ("sbuf", [128, 32], "int32"), "ri": ("sbuf", [128, 32], "int32"), "bi": ("sbuf", [128, 32], "int32"),
+    "cand": ("sbuf", [128, 64], "bfloat16"), "rz": ("sbuf", [128, 32], "float32"), "zz": ("sbuf", [128, 32], "float32"),
+    "dd": ("sbuf", [128, 32], "float32"), "le": ("sbuf", [128, 32], "float32"), "ee": ("sbuf", [128, 32], "bfloat16"),
+    "L": ("sbuf", [128, 16], "uint16"), "XL": ("sbuf", [128, 256], "float32"), "fr": ("sbuf", [128, 8], "float32"),
+    "E": ("sbuf", [128, 256], "bfloat16"), "off": ("sbuf", [128, 16], "uint16"),
+    "vals": ("sbuf", [128, 256], "bfloat16"), "old": ("sbuf", [128, 256], "bfloat16"),
+    "ob": ("sbuf", [128, 256], "float32"), "acc": ("sbuf", [128, 8], "float32"), "cb": ("sbuf", [128, 256], "float32"),
+    "ps": ("psum", [128, 4096], "float32"),
+}
+SEMAPHORES = (["cV", "cS", "cT", "cG", "stA", "stP", "stI", "ownA", "arrA", "arrP", "arrI", "arrN", "arrU", "sent",
+               "ldA", "ldW", "ldP", "ldI", "ldD", "ldE", "stN", "stU", "outN", "outU"] + ["w%d" % q for q in range(8)])
+
+A = AluOpType
+F = ActivationFunctionType
+
+
+def rank_program(g, core, T, topo):
+    me = T.rank_of(core)
+    if me is None:
+        return
+    cores = list(T.cores)
+    N = len(cores)
+    Q = {"V": g.vector, "S": g.scalar, "T": g.tensor, "G": g, "Y": g.sync}
+    total = {}
+    seen = {e: {} for e in Q}
+    wrote, read = {}, {}
+
+    def wait(e, tok):
+        if seen[e].get(tok[1], 0) < tok[2]:
+            Q[e].wait_ge(T.sem[tok[1]], tok[2])
+            seen[e][tok[1]] = tok[2]
+
+    def order(e, rd, wr):
+        for k in rd:
+            if k in wrote:
+                wait(e, wrote[k])
+        for k in wr:
+            if k in wrote and not (wrote[k][0] == e and (e == "T" or k[0] == "#")):
+                wait(e, wrote[k])
+            for tok in read.get(k, []):
+                if tok[0] != e:
+                    wait(e, tok)
+
+    def done(tok, rd, wr):
+        for k in rd:
+            read.setdefault(k, []).append(tok)
+        for k in wr:
+            wrote[k] = tok
+            read[k] = []
+
+    def op(e, rd, wr, call):
+        order(e, rd, wr)
+        s = "c" + e
+        total[s] = total.get(s, 0) + 1
+        call().then_inc(T.sem[s], 1)
+        done((e, s, total[s]), rd, wr)
+
+    def dmas(sem, items):
+        end = total.get(sem, 0) + 16 * len(items)
+        for e, out, src, rd, wr in items:
+            order(e, rd, wr)
+            Q[e].dma_start(out, src).then_inc(T.sem[sem], 16)
+        total[sem] = end
+        for e, out, src, rd, wr in items:
+            done(("dma", sem, end), rd, wr)
+
+    peers = [(me + d) % N for d in range(1, N)]
+    eng, used = {}, []
+    for q in sorted(peers, key=lambda q: len(topo.engines(core, cores[q]))):
+        free = [x for x in topo.engines(core, cores[q]) if x not in used]
+        pick = free[0] if topo.chip(core) != topo.chip(cores[q]) else free[-1]
+        eng[q] = pick
+        used.append(pick)
+
+    def exchange(src_of, dst, arr, rd, landed):
+        order("G", rd, [])
+        trs = []
+        for q in peers:
+            rid, pid, _ = topo.addr(cores[q])
+            trs.append(RemoteDMATransfer(dst_ids=[DstId(rid=rid, pnc=pid)], dma_engine_mask=1 << eng[q],
+                                         remote_sem=T.sem[arr], src=src_of(q), dst=dst))
+        g.remote_dma_fused(trs, local_sem=T.sem.sent)
+        total["sent"] = total.get("sent", 0) + len(peers)
+        total[arr] = len(peers)
+        wrote[landed] = ("far", arr, len(peers))
+
+    V, S, PE = g.vector, g.scalar, g.tensor
+
+    def ts(out, in0, s1, op0, rd, wr, s2=None, op1=None):
+        if op1 is None:
+            op("V", rd, wr, lambda: V.tensor_scalar(out, in0, s1, None, op0))
+        else:
+            op("V", rd, wr, lambda: V.tensor_scalar(out, in0, s1, s2, op0, op1))
+
+    def tt(out, in0, in1, o, rd, wr):
+        op("V", rd, wr, lambda: V.tensor_tensor(out, in0, in1, o))
+
+    def cp(out, in_, rd, wr):
+        op("V", rd, wr, lambda: V.tensor_copy(out, in_))
+
+    def fill(ap, c, wr):
+        op("V", [], wr, lambda: V.memset(ap, c))
+
+    def act(out, in_, fn, rd, wr, **kw):
+        op("S", rd, wr, lambda: S.activation(out, in_, fn, **kw))
+
+    def mm(out, lhsT, rhs, rd, bank, start=True, stop=True):
+        op("T", rd, ["#%d" % bank], lambda: PE.matmul(out, lhsT, rhs, start, stop))
+
+    def iota(out, pattern, base, cm, key, flt=True):
+        if flt:
+            op("G", [], [key], lambda: g.iota(out, pattern, base, cm, allow_small_or_imprecise_dtypes=True))
+        else:
+            op("G", [], [key], lambda: g.iota(out, pattern, base, cm))
+
+    def bank(b, lo=0, hi=512):
+        return T.ps[:, 512 * b + lo:512 * b + hi]
+
+    dmas("stA", [("Y", T.SA[:, 0:64, :], T.part[:], [], ["SA"]), ("S", T.SA[:, 64:128, :], T.w[:], [], ["SA2"])])
+    dmas("ownA", [("Y", T.LA[me, 0:64, :], T.part[me:me + 1, :], [], ["LAo"]),
+                  ("S", T.LA[me, 64:128, :], T.w[me:me + 1, :], [], ["LAo2"])])
+    dmas("stP", [("Y" if i % 2 else "S", T.SP[:, 16 * i:16 * i + 16, :], T.pin[:, 64 * i:64 * i + 64], [], ["SP%d" % i])
+                 for i in range(8)])
+    dmas("stI", [("Y" if t else "S", T.SI[:, 16 * i:16 * i + 16, 32 * t:32 * t + 32], T.inc[t::2, 64 * i:64 * i + 64],
+                  [], ["SI%d%d" % (i, t)]) for i in range(8) for t in range(2)])
+
+    iota(T.kI[:, 0:1], [[0, 1]], 0, 1, "k", flt=False)
+    iota(T.i32[:], [[1, 32]], 0, 0, "i32")
+    iota(T.pM[:], [[0, 8], [1, 16]], 0, 0, "pM")
+    iota(T.im[:], [[1, 128]], 0, -1, "im")
+    exchange(lambda q: T.SA[q], T.LA[me], "arrA", ["SA"], "LA")
+    exchange(lambda q: T.SP[q], T.LP[me], "arrP", ["SP0"], "LP")
+    iota(T.iM[:], [[1, 8], [0, 16]], 0, 0, "iM")
+    iota(T.iK[:], [[1, 32]], 1024, 0, "iK")
+    exchange(lambda q: T.SI[q], T.LI[me], "arrI", ["SI00"], "LI")
+    for t in range(2):
+        for h in range(2):
+            c = 32 * t + 16 * h
+            iota(T.posb[:, c:c + 16], [[64, 2], [16, 2], [0, 4]], 32 + 32 * t + 1024 * h, 0, "posb%d" % c)
+    iota(T.Di[:, 0:32], [[1, 32]], -PAD, 2, "Dpad", flt=False)
+
+    kF = T.kF
+    i16 = T.i32[:, 0:16]
+
+    def col(j):
+        return kF[:, j:j + 1]
+
+    def blk(j):
+        return T.f[:, 16 * j:16 * j + 16]
+
+    fill(T.Di[:, 32:1056], 0, ["Dz0"])
+    ts(T.kI[:, 1:2], T.kI[:, 0:1], 15, A.bitwise_and, ["k"], ["k1"])
+    ts(T.kI[:, 2:3], T.kI[:, 0:1], 4, A.arith_shift_right, ["k"], ["k2"])
+    ts(T.kI[:, 3:4], T.kI[:, 0:1], 7, A.bitwise_and, ["k"], ["k3"])
+    ts(T.kI[:, 4:5], T.kI[:, 0:1], 3, A.arith_shift_right, ["k"], ["k4"])
+    ts(T.kI[:, 5:6], T.kI[:, 0:1], 31, A.bitwise_and, ["k"], ["k5"])
+    ts(T.onesm[:], T.pM[:], 15.0, A.not_equal, ["pM"], ["onesm"])
+    cp(kF[:, 0:6], T.kI[:, 0:6], ["k", "k1", "k2", "k3", "k4", "k5"], ["kF"])
+    ts(T.Id32[:], T.i32[:], col(0), A.is_equal, ["i32", "kF"], ["Id32"])
+    fill(T.Di[:, 1056:DW], 0, ["Dz1"])
+    c15, c127, z0, cm, pc, b0, spec, bias = [col(j) for j in range(8, 16)]
+    ts(c15, col(0), 15.0, A.is_equal, ["kF"], ["c15"])
+    ts(c127, col(0), 127.0, A.is_equal, ["kF"], ["c127"])
+    ts(z0, col(1), 0.0, A.is_equal, ["kF"], ["z0"])
+    ts(cm, col(1), 15.0, A.not_equal, ["kF"], ["cm"], -16.0, A.mult)
+    ts(pc, col(3), 128.0, A.mult, ["kF"], ["pc"], col(4), A.add)
+    ts(blk(0), i16, col(1), A.subtract, ["i32", "kF"], ["d"])
+    ts(T.Q8[:], T.i32[:, 0:8], col(2), A.is_equal, ["i32", "kF"], ["Q8"])
+    ts(T.SelS[:], i16, col(1), A.is_equal, ["i32", "kF"], ["SelS"], 32.0, A.mult)
+    ts(b0, col(1), cm, A.mult, ["kF", "cm"], ["b0"], 0.0625, A.mult)
+    tt(spec, c15, c127, A.add, ["c15", "c127"], ["spec"])
+    tt(blk(1), blk(0), blk(0), A.mult, ["d"], ["d2"])
+    ts(blk(2), blk(0), 0.0, A.is_equal, ["d"], ["a0"], -2.0, A.mult)
+    ts(blk(3), i16, 0.0, A.is_equal, ["i32", "c15"], ["p0"], c15, A.mult)
+    ts(blk(4), i16, 16.0, A.add, ["i32", "c15"], ["p16"], c15, A.mult)
+    tt(bias, b0, c15, A.add, ["b0", "c15"], ["bias"])
+    ts(blk(5), blk(1), 1.0, A.is_equal, ["d2"], ["a1"])
+    ts(T.NE[:], T.i32[:, 0:8], col(2), A.not_equal, ["i32", "kF", "spec"], ["NE"], spec, A.max)
+    ts(blk(6), blk(3), -128.0, A.mult, ["p0"], ["pC"], c127, A.add)
+    ts(blk(7), blk(3), -112.0, A.mult, ["p0"], ["pZ"], c127, A.add)
+    ts(blk(8), blk(3), -16.0, A.mult, ["p0"], ["pO"])
+    tt(blk(9), blk(5), blk(2), A.add, ["a1", "a0"], ["F"])
+    tt(blk(10), blk(8), blk(4), A.add, ["pO", "p16"], ["pO2"])
+    ts(T.Idb[:], T.im[:], 0.0, A.is_equal, ["im"], ["Idb"])
+    ts(T.f[:, 144:145], T.f[:, 144:145], z0, A.add, ["F", "z0"], ["F"])
+    ts(T.t0[:], T.im[:], 0.0, A.is_gt, ["im"], ["t0"])
+    ts(T.t1[:], T.im[:], 0.0, A.is_equal, ["im"], ["t1"], 1024.0, A.mult)
+    ts(blk(11), blk(9), cm, A.mult, ["F", "cm"], ["Fm"])
+    tt(T.TB[:], T.t0[:], T.t1[:], A.add, ["t0", "t1"], ["TB"])
+    tt(T.LC[:], blk(11), blk(6), A.add, ["Fm", "pC"], ["LC"])
+    tt(T.LO[:], blk(11), blk(10), A.add, ["Fm", "pO2"], ["LO"])
+    tt(blk(12), blk(11), blk(7), A.add, ["Fm", "pZ"], ["FZ"])
+    fill(T.onesb[:], 1.0, ["onesb"])
+    fill(T.onesf[:], 1.0, ["onesf"])
+    fill(T.cand[:], 0.0, ["cand0", "cand1"])
+    fill(T.G[:, 0:PAD], 0.0, ["Gpad"])
+    fill(T.acc[:], 0.0, ["acc0", "acc1", "acc2", "acc3", "acc4"])
+    fill(T.cb[0:1, :], 0.0, ["cb"])
+    for i in range(8):
+        ts(T.LZ[:, 16 * i:16 * i + 16], blk(12), T.NE[:, i:i + 1], A.mult, ["FZ", "NE"], ["LZ%d" % i])
+    for x in range(2):
+        ts(T.reset[:, 128 * x:128 * x + 128], T.pM[:], 0.0, A.is_equal, ["pM"], ["reset%d" % x], 1048576.0, A.mult)
+    ts(T.maskR[:], T.iM[:], col(1), A.is_equal, ["iM", "kF"], ["maskR"])
+    ts(T.posc[:], T.posb[:], pc, A.add, ["posb0", "posb16", "posb32", "posb48", "pc"], ["posc"], -0.5, A.add)
+    LZk = ["LZ%d" % i for i in range(8)]
+
+    for j in range(32):
+        act(T.Sel[0:32, 128 * j:128 * j + 128], T.onesm[0:32, :], F.Identity, ["onesm", "Id32"], ["Sel%d" % j],
+            scale=T.Id32[0:32, j:j + 1])
+
+    dmas("ldA", [("Y", T.Ai[0:32, :], T.LA[:, 0:64, :], ["LA", "LAo"], ["Ai"])])
+    dmas("ldW", [("Y", T.Wi[0:32, :], T.LA[:, 64:128, :], ["LA", "LAo"], ["Wi"])])
+    first = [me] + peers
+    dmas("ldP", [("Y", T.pinI[:, 64 * q:64 * q + 64], T.SP[q] if q == me else T.LP[q], ["SP0"] if q == me else ["LP"],
+                  ["pinI%d" % q]) for q in first])
+    dmas("ldI", [("Y", T.incI[:, 64 * q:64 * q + 64], T.SI[q] if q == me else T.LI[q], ["SI00"] if q == me else ["LI"],
+                  ["incI%d" % q]) for q in first])
+    for kh, e, sem in ((0, "Y", "ldE"), (1, "G", "ldD")):
+        dmas(sem, [(e, T.Di[32 * (q % 4) + 16 * kh:32 * (q % 4) + 16 * kh + 8, 32 + 1024 * (q // 4):1056 + 1024 * (q // 4)],
+                    T.SI[q] if q == me else T.LI[q], ["SI00" if q == me else "LI", "Dz0", "Dz1"], ["D%d%d" % (kh, q)])
+                   for q in first])
+
+    cp(T.Ab[0:32, :], T.Ai[0:32, :], ["Ai"], ["Ab"])
+    cp(T.Wb[0:32, :], T.Wi[0:32, :], ["Wi"], ["Wb"])
+    for j in range(16):
+        b = j % 8
+        for x in range(2):
+            r = 2 * j + x
+            mm(bank(b, 256 * x, 256 * x + 256), T.Sel[0:32, 128 * r:128 * r + 128], T.Ab[0:32, :], ["Sel%d" % r, "Ab"], b)
+        out = T.win[:, 512 * j:512 * j + 512]
+        if j % 2 and j < 15:
+            ts(out, bank(b), bias, A.add, ["bias"], ["#%d" % b, "win%d" % j], 0.0, A.max)
+        else:
+            act(out, bank(b), F.Relu, ["bias"], ["#%d" % b, "win%d" % j], bias=bias)
+    wink = ["win%d" % j for j in range(16)]
+    cp(T.pinU[:], T.pinI[:], ["pinI0"], ["pinU"])
+    for t in range(2):
+        for h in range(2):
+            for jj in range(4):
+                c = 32 * t + 16 * h + 4 * jj
+                mm(bank(1, c, c + 4), T.Ab[0:32, t:256:2], T.Idb[0:32, 16 * h + jj:16 * h + 16:4], ["Ab", "Idb"], 1)
+    cp(T.own[:], bank(1, 0, 64), [], ["#1", "own"])
+
+    for q in range(8):
+        out = T.G[:, PAD + 1024 * q:PAD + 1024 * q + 1024]
+        src = T.win[:, 0:NV].indirect(T.pinU[:, 64 * q:64 * q + 64])
+        if q % 2 == 0:
+            cp(out, src, wink + ["pinU"], ["G%d" % q])
+        else:
+            act(out, src, F.Copy, wink + ["pinU"], ["G%d" % q])
+        dmas("w%d" % q, [("Y", T.G[127:128, PAD + 1024 * q:PAD + 1024 * q + 1024], T.Wb[4 * q:4 * q + 4, :], ["Wb"], ["G%d" % q])])
+    Gk = ["G%d" % q for q in range(8)]
+    Zk = ["Z%d" % j for j in range(16)]
+    Dk = ["D00", "D10", "Dpad"]
+    cp(T.incU[:], T.incI[:], ["incI0"], ["incU"])
+
+    def gather_y(t, q, e, lo=0, hi=32):
+        out = T.Y[:, 512 * q + 16 * lo:512 * q + 16 * hi]
+        src = T.Z[:, 0:NV].indirect(T.incU[:, 64 * q + 32 * t + lo:64 * q + 32 * t + hi])
+        keys = ["Y%d%d" % (q, b) for b in range(lo // 16, hi // 16)]
+        if e == "S":
+            act(out, src, F.Copy, Zk + ["incU"], keys)
+        else:
+            cp(out, src, Zk + ["incU"], keys)
+
+    def keys_of(t, q):
+        for jj in (0, 2, 1, 3):
+            c = 16 * (4 * jj + q % 4)
+            u = 1024 * q + 256 * jj
+            n = 512 * q + 256 * (jj & 1)
+            mm(bank(q // 4, c, c + 16), T.win[0:16, u + t:u + 256:2], T.LO[0:16, :], wink + ["LO"], q // 4, True, False)
+            mm(bank(q // 4, c, c + 16), T.Y[:, n + (jj >> 1):n + 256:2], T.SelS[:], ["Y%d%d" % (q, jj & 1), "SelS"], q // 4,
+               False, True)
+
+    def chain(t, h):
+        H = str(h)
+        c, w = slice(16 * h, 16 * h + 16), slice(128 * h, 128 * h + 128)
+        bp, bz, bo, bv = 2 + h, 4 + h, h, 6
+        mins = T.mins[:, 256 * h:256 * h + 256]
+        op("V", ["reset0", "reset1"], ["#" + H, "mins" + H],
+           lambda: V.tensor_tensor_scan(mins, T.reset[:], bank(h, 0, 256), 0.0, A.add, A.min))
+        yield
+        cp(T.ki[:, c], T.mins[:, 256 * h + 15:256 * h + 256:16], ["mins" + H], ["ki" + H])
+        yield
+        ts(T.ri[:, c], T.ki[:, c], 31, A.bitwise_and, ["ki" + H], ["ri" + H])
+        yield
+        ts(T.cand[:, 32 * h + 12:32 * h + 28], T.ri[:, c], 16.0, A.is_ge, ["ri" + H], ["cand" + H])
+        ts(T.rz[:, c], T.ri[:, c], 0.03125, A.mult, ["ri" + H], ["rz" + H])
+        for s in range(4):
+            mm(bank(bp, 0, 16), T.TB[:] if s == 0 else T.onesb[:], T.cand[:, 32 * h + 12 - 4 * s:32 * h + 28 - 4 * s],
+               ["cand" + H, "TB", "onesb"], bp, s == 0, s == 3)
+        tt(T.zz[:, c], T.rz[:, c], T.posc[:, 32 * t + 16 * h:32 * t + 16 * h + 16], A.add, ["rz" + H, "posc"], ["zz" + H])
+        yield
+        for jj in range(4):
+            for q in range(4):
+                j = 4 * jj + q
+                ts(T.P[:, 512 * h + 32 * j:512 * h + 32 * j + 32], T.iK[:], bank(bp, j, j + 1), A.is_equal, ["iK", "zz" + H],
+                   ["#%d" % bp, "P%d_%d" % (h, j)], T.zz[:, 16 * h + j:16 * h + j + 1], A.mult)
+            mm(bank(bz, 0, 8), T.P[:, 512 * h + 128 * jj:512 * h + 128 * jj + 128], T.onesf[:],
+               ["P%d_%d" % (h, 4 * jj + q) for q in range(4)] + ["onesf"], bz, jj == 0, jj == 3)
+            yield
+        L = T.L[:, 8 * h:8 * h + 8]
+        ts(L, bank(bz, 0, 8), col(5), A.max, ["kF"], ["#%d" % bz, "L" + H])
+        yield
+        tt(T.XL[:, w], T.Di[:, 0:DW].indirect(L), T.maskR[:], A.mult, Dk + ["L" + H, "maskR"], ["XL" + H])
+        mm(bank(bo, 256, 264), T.XL[:, w], T.Q8[:], ["XL" + H, "Q8"], bo)
+        yield
+        fr = T.fr[:, 4 * h:4 * h + 1]
+        ts(fr, T.L[:, 8 * h:8 * h + 1], bank(bz, 0, 1), A.subtract, ["L" + H], ["#%d" % bz, "fr" + H], -32.0, A.mult)
+        act(T.E[:, w], T.Idb[:], F.Identity, ["Idb", "fr" + H], ["E" + H], scale=fr)
+        mm(bank(bv, 0, 128), T.onesm[:], T.E[:, w], ["onesm", "E" + H], bv)
+        act(T.vals[:, w], bank(bv, 0, 128), F.Relu, ["bias"], ["#%d" % bv, "vals" + H], bias=bias)
+        yield
+        off = T.off[:, 8 * h:8 * h + 8]
+        ts(off, bank(bo, 256, 264), float(PAD), A.add, [], ["#%d" % bo, "off" + H])
+        yield
+        act(T.old[:, w], T.G[:, 0:PAD + NV].indirect(off), F.Identity, Gk + ["Gpad", "off" + H, "c127"], ["old" + H], scale=c127)
+        yield
+        tt(T.G[:, 0:PAD + NV].indirect(off), T.old[:, w], T.vals[:, w], A.add, ["old" + H, "vals" + H, "off" + H], Gk + ["Gpad"])
+        yield
+
+    def third(t):
+        gather_y(t, 4, "V", 0, 16)
+        yield
+        gather_y(t, 4, "V", 16, 32)
+        yield
+        keys_of(t, 4)
+        yield
+
+    def later(t):
+        for q in (5, 6, 7):
+            keys_of(t, q)
+            yield
+
+    def new_rows(t):
+        pn = T.ps[0:32, 512 * 7:512 * 7 + 128]
+        mm(pn, T.ee[:], T.Idb[:], ["ee", "Idb"], 7, True, False)
+        mm(pn, T.own[:, 32 * t:32 * t + 32], T.Idb[:], ["own", "Idb"], 7, False, True)
+        act(T.ob[0:32, t:256:2], pn, F.Copy, [], ["#7", "ob%d" % t])
+
+    for t in range(2):
+        for j in range(16):
+            b = j % 8
+            mm(bank(b), T.LZ[:], T.G[:, PAD + 512 * j:PAD + 512 * j + 512], LZk + ["G%d" % (j // 2)], b)
+            out = T.Z[:, 512 * j:512 * j + 512]
+            if t == 1 and j == 2:
+                new_rows(0)
+            if j % 2 and (j < 15 or t == 1):
+                ts(out, bank(b), 0.0, A.max, [], ["#%d" % b, "Z%d" % j])
+            else:
+                act(out, bank(b), F.Relu, [], ["#%d" % b, "Z%d" % j])
+        for q, e in ((0, "V"), (2, "S"), (1, "V"), (3, "S")):
+            gather_y(t, q, e, 0, 16)
+            gather_y(t, q, e, 16, 32)
+            keys_of(t, q)
+        for q in (5, 6, 7):
+            gather_y(t, q, "S")
+        if t == 0:
+            act(T.junk[0:32, :], T.Wb[0:32, :], F.Identity, ["Wb"], ["junk", "acc4"], scale=-15.0, accum_out=T.acc[0:32, 4:5])
+        steps = {"a": chain(t, 0), "b": chain(t, 1), "x": third(t), "k": later(t)}
+        for ch in ORDER:
+            next(steps[ch], None)
+        for h in range(2):
+            ts(T.le[:, 16 * h:16 * h + 16], bank(2 + h, 0, 16), 1055.5, A.is_le, [], ["#%d" % (2 + h), "le%d" % h])
+        ts(T.bi[:], T.ki[:], 15, A.bitwise_and, ["ki0", "ki1"], ["bi"])
+        tt(T.dd[:], T.bi[:], T.own[:, 32 * t:32 * t + 32], A.subtract, ["bi", "own"], ["dd"])
+        tt(T.ee[:], T.le[:], T.dd[:], A.mult, ["le0", "le1", "dd"], ["ee"])
+
+    for r in range(4):
+        for x in range(16):
+            e0 = PAD + 128 * (16 * r + x)
+            mm(bank(r, 16 * x, 16 * x + 16), T.G[:, e0:e0 + 128], T.LC[:], Gk + ["LC"], r)
+        act(T.junk[:], bank(r, 0, 256), F.Relu, [], ["#%d" % r, "junk", "acc%d" % r], accum_out=T.acc[:, r:r + 1])
+        if r == 0:
+            new_rows(1)
+            dmas("stN", [("Y", T.SN[4 * h:4 * h + 4, 32 * jj:32 * jj + 32, :], T.ob[16 * h + 4 * jj:16 * h + 4 * jj + 4, :],
+                          ["ob0", "ob1"], ["SN%d%d" % (h, jj)]) for h in range(2) for jj in range(4)])
+            exchange(lambda q: T.SN[q], T.LN[me], "arrN", ["SN00"], "LN")
+    pcut = T.ps[0:1, 512 * 6:512 * 6 + 8]
+    mm(pcut, T.onesf[:, 0:1], T.acc[:], ["onesf", "acc0", "acc1", "acc2", "acc3", "acc4"], 6)
+    op("V", [], ["#6", "cb"], lambda: V.tensor_reduce(T.cb[0:1, 0:1], pcut, AxisListType.X, A.add, negate=True))
+    dmas("stU", [("S", T.SU[:], T.cb[0:1, :], ["cb"], ["SU"])])
+    exchange(lambda q: T.SU[:], T.LU[me], "arrU", ["SU"], "LU")
+
+    outs = [("Y", T.newpart[me:me + 1, :], T.SN[me], ["SN00"], ["o0"])]
+    if me > 0:
+        outs.append(("Y", T.newpart[0:me, :], T.LN[0:me], ["LN"], ["o1"]))
+    if me < N - 1:
+        outs.append(("Y", T.newpart[me + 1:N, :], T.LN[me + 1:N], ["LN"], ["o2"]))
+    dmas("outN", outs)
+    dmas("outU", [("S", T.cut[me:me + 1, :], T.cb[0:1, 0:1], ["cb"], ["u"])]
+         + [("Y" if n % 2 == 0 else "S", T.cut[q:q + 1, :], T.LU[q, 0:1, 0:1], ["LU"], ["u%d" % q]) for n, q in enumerate(peers)])
+    for s in total:
+        g.wait_ge(T.sem[s], total[s])

@@ -4,25 +4,30 @@ from concourse.mybir import AluOpType, AxisListType, ActivationFunctionType
 PAD = 288
 NV = 8192
 DW = 32 + 2048
-ORDER = "xxakaaaxkaakaabababbabbbbabbababbb"
+BATCH = (((0, 1, 2, 3), 0, 0, 0), ((4, 5, 6, 7), 1, 0, 16))
+ORDER = "vsvsvsv" "AsvAAAAssAAsAAx" "BBaBBaBaBBBBxabbbabxb"
+PIECES = {"V": ((0, (0, 1)), (2, (0,)), (2, (1,)), (4, (0,)), (4, (1,))),
+          "S": ((1, (0, 1)), (3, (0,)), (3, (1,)), (5, (0, 1)), (6, (0, 1)), (7, (0,)), (7, (1,)))}
+CUT = (20, 20, 16, 8)
 
 SCRATCH = {
-    "SA": ("dram", [8, 128, 16], "int32"), "LA": ("dram", [8, 128, 16], "int32"),
+    "SA": ("dram", [8, 128, 8], "int32"), "LA": ("dram", [8, 128, 8], "int32"),
+    "SW": ("dram", [8, 128, 8], "bfloat16"), "LW": ("dram", [8, 128, 8], "bfloat16"),
     "SP": ("dram", [8, 128, 64], "int32"), "LP": ("dram", [8, 128, 64], "int32"),
     "SI": ("dram", [8, 128, 64], "int32"), "LI": ("dram", [8, 128, 64], "int32"),
     "SN": ("dram", [8, 128, 8], "float32"), "LN": ("dram", [8, 128, 8], "float32"),
     "SU": ("dram", [128, 2], "float32"), "LU": ("dram", [8, 128, 2], "float32"),
     "win": ("sbuf", [128, NV], "bfloat16"), "G": ("sbuf", [128, PAD + NV], "bfloat16"),
     "Z": ("sbuf", [128, NV], "bfloat16"), "Y": ("sbuf", [128, 4096], "bfloat16"),
-    "Di": ("sbuf", [128, DW], "int32"), "P": ("sbuf", [128, 1024], "float32"),
+    "Di": ("sbuf", [128, DW], "int32"), "P": ("sbuf", [128, 1536], "float32"),
     "pinI": ("sbuf", [128, 512], "int32"), "incI": ("sbuf", [128, 512], "int32"),
     "pinU": ("sbuf", [128, 512], "uint16"), "incU": ("sbuf", [128, 512], "uint16"),
-    "Ai": ("sbuf", [128, 256], "int32"), "Wi": ("sbuf", [128, 256], "int32"),
-    "Ab": ("sbuf", [128, 256], "bfloat16"), "Wb": ("sbuf", [128, 256], "bfloat16"),
-    "junk": ("sbuf", [128, 256], "bfloat16"),
-    "Sel": ("sbuf", [128, 4096], "bfloat16"), "reset": ("sbuf", [128, 256], "float32"),
+    "Ai": ("sbuf", [128, 256], "int32"), "Wi": ("sbuf", [128, 256], "int32"), "Ao": ("sbuf", [128, 256], "int32"),
+    "Ab": ("sbuf", [128, 256], "bfloat16"), "Wb": ("sbuf", [128, 256], "bfloat16"), "Aob": ("sbuf", [128, 256], "bfloat16"),
+    "Wl": ("sbuf", [128, 256], "bfloat16"), "junk": ("sbuf", [128, 320], "bfloat16"),
+    "Sel": ("sbuf", [128, 4096], "bfloat16"), "reset": ("sbuf", [128, 256], "float32"), "pK": ("sbuf", [128, 256], "bfloat16"),
     "kI": ("sbuf", [128, 8], "int32"), "kF": ("sbuf", [128, 32], "float32"),
-    "im": ("sbuf", [128, 128], "float32"), "iM": ("sbuf", [128, 128], "float32"), "pM": ("sbuf", [128, 128], "float32"),
+    "im": ("sbuf", [128, 128], "float32"), "iM": ("sbuf", [128, 128], "float32"), "pM": ("sbuf", [128, 256], "float32"),
     "i32": ("sbuf", [128, 32], "float32"), "iK": ("sbuf", [128, 32], "float32"), "posc": ("sbuf", [128, 64], "float32"),
     "posb": ("sbuf", [128, 64], "float32"),
     "Idb": ("sbuf", [128, 128], "bfloat16"), "Id32": ("sbuf", [128, 32], "float32"), "TB": ("sbuf", [128, 128], "bfloat16"),
@@ -31,18 +36,19 @@ SCRATCH = {
     "maskR": ("sbuf", [128, 128], "float32"), "Q8": ("sbuf", [128, 8], "float32"), "NE": ("sbuf", [128, 8], "float32"),
     "SelS": ("sbuf", [128, 16], "bfloat16"), "LZ": ("sbuf", [128, 128], "bfloat16"),
     "LC": ("sbuf", [128, 16], "bfloat16"), "LO": ("sbuf", [128, 16], "bfloat16"), "f": ("sbuf", [128, 256], "float32"),
-    "own": ("sbuf", [128, 64], "bfloat16"), "mins": ("sbuf", [128, 512], "float32"),
-    "ki": ("sbuf", [128, 32], "int32"), "ri": ("sbuf", [128, 32], "int32"), "bi": ("sbuf", [128, 32], "int32"),
-    "cand": ("sbuf", [128, 64], "bfloat16"), "rz": ("sbuf", [128, 32], "float32"), "zz": ("sbuf", [128, 32], "float32"),
-    "dd": ("sbuf", [128, 32], "float32"), "le": ("sbuf", [128, 32], "float32"), "ee": ("sbuf", [128, 32], "bfloat16"),
-    "L": ("sbuf", [128, 16], "uint16"), "XL": ("sbuf", [128, 256], "float32"), "fr": ("sbuf", [128, 8], "float32"),
-    "E": ("sbuf", [128, 256], "bfloat16"), "off": ("sbuf", [128, 16], "uint16"),
-    "vals": ("sbuf", [128, 256], "bfloat16"), "old": ("sbuf", [128, 256], "bfloat16"),
+    "own": ("sbuf", [128, 64], "bfloat16"), "own32": ("sbuf", [128, 64], "float32"), "mins": ("sbuf", [128, 512], "float32"),
+    "xi": ("sbuf", [128, 32], "int32"), "cand": ("sbuf", [128, 96], "bfloat16"), "rr": ("sbuf", [128, 64], "float32"),
+    "zz": ("sbuf", [128, 32], "float32"), "dd": ("sbuf", [128, 64], "bfloat16"), "le": ("sbuf", [128, 64], "float32"),
+    "ee": ("sbuf", [128, 64], "bfloat16"), "Id16": ("sbuf", [128, 128], "bfloat16"),
+    "L": ("sbuf", [128, 24], "uint16"), "XL": ("sbuf", [128, 384], "float32"), "fr": ("sbuf", [128, 8], "float32"),
+    "E": ("sbuf", [128, 384], "bfloat16"), "off": ("sbuf", [128, 24], "uint16"),
+    "vals": ("sbuf", [128, 384], "bfloat16"), "old": ("sbuf", [128, 384], "bfloat16"),
     "ob": ("sbuf", [128, 256], "float32"), "acc": ("sbuf", [128, 8], "float32"), "cb": ("sbuf", [128, 256], "float32"),
     "ps": ("psum", [128, 4096], "float32"),
 }
-SEMAPHORES = (["cV", "cS", "cT", "cG", "stA", "stP", "stI", "ownA", "arrA", "arrP", "arrI", "arrN", "arrU", "sent",
-               "ldA", "ldW", "ldP", "ldI", "ldD", "ldE", "stN", "stU", "outN", "outU"] + ["w%d" % q for q in range(8)])
+SEMAPHORES = (["cV", "cS", "cT", "cG", "stA", "stP", "stI", "stW", "ownA", "arrA", "arrP", "arrW", "arrI", "arrN", "arrU", "sent",
+               "ldO", "ldV", "ldA", "ldW", "ldP", "ldI0", "ldI1", "ldD", "stN", "stU", "outN", "outU"]
+              + ["w%d" % q for q in range(8)])
 
 A = AluOpType
 F = ActivationFunctionType
@@ -54,6 +60,7 @@ def rank_program(g, core, T, topo):
         return
     cores = list(T.cores)
     N = len(cores)
+    NB = len(BATCH)
     Q = {"V": g.vector, "S": g.scalar, "T": g.tensor, "G": g, "Y": g.sync}
     total = {}
     seen = {e: {} for e in Q}
@@ -150,28 +157,19 @@ def rank_program(g, core, T, topo):
     def bank(b, lo=0, hi=512):
         return T.ps[:, 512 * b + lo:512 * b + hi]
 
-    dmas("stA", [("Y", T.SA[:, 0:64, :], T.part[:], [], ["SA"]), ("S", T.SA[:, 64:128, :], T.w[:], [], ["SA2"])])
-    dmas("ownA", [("Y", T.LA[me, 0:64, :], T.part[me:me + 1, :], [], ["LAo"]),
-                  ("S", T.LA[me, 64:128, :], T.w[me:me + 1, :], [], ["LAo2"])])
+    dmas("stA", [("Y", T.SA[:], T.part[:], [], ["SA"])])
+    dmas("ldO", [("Y", T.Ao[0:4, :], T.part[me:me + 1, :], [], ["Ao"])])
+    dmas("ldV", [("S", T.Wi[0:32, :], T.w[:], [], ["Wi"])])
+    dmas("ownA", [("S", T.LA[me], T.part[me:me + 1, :], [], ["LAo"])])
     dmas("stP", [("Y" if i % 2 else "S", T.SP[:, 16 * i:16 * i + 16, :], T.pin[:, 64 * i:64 * i + 64], [], ["SP%d" % i])
                  for i in range(8)])
-    dmas("stI", [("Y" if t else "S", T.SI[:, 16 * i:16 * i + 16, 32 * t:32 * t + 32], T.inc[t::2, 64 * i:64 * i + 64],
-                  [], ["SI%d%d" % (i, t)]) for i in range(8) for t in range(2)])
 
     iota(T.kI[:, 0:1], [[0, 1]], 0, 1, "k", flt=False)
     iota(T.i32[:], [[1, 32]], 0, 0, "i32")
-    iota(T.pM[:], [[0, 8], [1, 16]], 0, 0, "pM")
+    iota(T.pM[:], [[0, 16], [1, 16]], 0, 0, "pM")
     iota(T.im[:], [[1, 128]], 0, -1, "im")
     exchange(lambda q: T.SA[q], T.LA[me], "arrA", ["SA"], "LA")
     exchange(lambda q: T.SP[q], T.LP[me], "arrP", ["SP0"], "LP")
-    iota(T.iM[:], [[1, 8], [0, 16]], 0, 0, "iM")
-    iota(T.iK[:], [[1, 32]], 1024, 0, "iK")
-    exchange(lambda q: T.SI[q], T.LI[me], "arrI", ["SI00"], "LI")
-    for t in range(2):
-        for h in range(2):
-            c = 32 * t + 16 * h
-            iota(T.posb[:, c:c + 16], [[64, 2], [16, 2], [0, 4]], 32 + 32 * t + 1024 * h, 0, "posb%d" % c)
-    iota(T.Di[:, 0:32], [[1, 32]], -PAD, 2, "Dpad", flt=False)
 
     kF = T.kF
     i16 = T.i32[:, 0:16]
@@ -188,92 +186,119 @@ def rank_program(g, core, T, topo):
     ts(T.kI[:, 3:4], T.kI[:, 0:1], 7, A.bitwise_and, ["k"], ["k3"])
     ts(T.kI[:, 4:5], T.kI[:, 0:1], 3, A.arith_shift_right, ["k"], ["k4"])
     ts(T.kI[:, 5:6], T.kI[:, 0:1], 31, A.bitwise_and, ["k"], ["k5"])
-    ts(T.onesm[:], T.pM[:], 15.0, A.not_equal, ["pM"], ["onesm"])
+    ts(T.onesm[:], T.pM[:, 0:128], 15.0, A.not_equal, ["pM"], ["onesm"])
     cp(kF[:, 0:6], T.kI[:, 0:6], ["k", "k1", "k2", "k3", "k4", "k5"], ["kF"])
+    fill(T.onesb[:], 1.0, ["onesb"])
     ts(T.Id32[:], T.i32[:], col(0), A.is_equal, ["i32", "kF"], ["Id32"])
-    fill(T.Di[:, 1056:DW], 0, ["Dz1"])
-    c15, c127, z0, cm, pc, b0, spec, bias = [col(j) for j in range(8, 16)]
+    c15, c127, z0, cm, pc, b0, spec, bias, bias2, lim = [col(j) for j in range(8, 18)]
     ts(c15, col(0), 15.0, A.is_equal, ["kF"], ["c15"])
+    ts(cm, col(1), 15.0, A.not_equal, ["kF"], ["cm"], -16.0, A.mult)
     ts(c127, col(0), 127.0, A.is_equal, ["kF"], ["c127"])
     ts(z0, col(1), 0.0, A.is_equal, ["kF"], ["z0"])
-    ts(cm, col(1), 15.0, A.not_equal, ["kF"], ["cm"], -16.0, A.mult)
+    ts(b0, col(1), cm, A.mult, ["kF", "cm"], ["b0"], 0.0625, A.mult)
     ts(pc, col(3), 128.0, A.mult, ["kF"], ["pc"], col(4), A.add)
     ts(blk(0), i16, col(1), A.subtract, ["i32", "kF"], ["d"])
-    ts(T.Q8[:], T.i32[:, 0:8], col(2), A.is_equal, ["i32", "kF"], ["Q8"])
-    ts(T.SelS[:], i16, col(1), A.is_equal, ["i32", "kF"], ["SelS"], 32.0, A.mult)
-    ts(b0, col(1), cm, A.mult, ["kF", "cm"], ["b0"], 0.0625, A.mult)
-    tt(spec, c15, c127, A.add, ["c15", "c127"], ["spec"])
-    tt(blk(1), blk(0), blk(0), A.mult, ["d"], ["d2"])
-    ts(blk(2), blk(0), 0.0, A.is_equal, ["d"], ["a0"], -2.0, A.mult)
-    ts(blk(3), i16, 0.0, A.is_equal, ["i32", "c15"], ["p0"], c15, A.mult)
-    ts(blk(4), i16, 16.0, A.add, ["i32", "c15"], ["p16"], c15, A.mult)
     tt(bias, b0, c15, A.add, ["b0", "c15"], ["bias"])
-    ts(blk(5), blk(1), 1.0, A.is_equal, ["d2"], ["a1"])
-    ts(T.NE[:], T.i32[:, 0:8], col(2), A.not_equal, ["i32", "kF", "spec"], ["NE"], spec, A.max)
-    ts(blk(6), blk(3), -128.0, A.mult, ["p0"], ["pC"], c127, A.add)
-    ts(blk(7), blk(3), -112.0, A.mult, ["p0"], ["pZ"], c127, A.add)
-    ts(blk(8), blk(3), -16.0, A.mult, ["p0"], ["pO"])
-    tt(blk(9), blk(5), blk(2), A.add, ["a1", "a0"], ["F"])
-    tt(blk(10), blk(8), blk(4), A.add, ["pO", "p16"], ["pO2"])
-    ts(T.Idb[:], T.im[:], 0.0, A.is_equal, ["im"], ["Idb"])
-    ts(T.f[:, 144:145], T.f[:, 144:145], z0, A.add, ["F", "z0"], ["F"])
-    ts(T.t0[:], T.im[:], 0.0, A.is_gt, ["im"], ["t0"])
-    ts(T.t1[:], T.im[:], 0.0, A.is_equal, ["im"], ["t1"], 1024.0, A.mult)
-    ts(blk(11), blk(9), cm, A.mult, ["F", "cm"], ["Fm"])
-    tt(T.TB[:], T.t0[:], T.t1[:], A.add, ["t0", "t1"], ["TB"])
-    tt(T.LC[:], blk(11), blk(6), A.add, ["Fm", "pC"], ["LC"])
-    tt(T.LO[:], blk(11), blk(10), A.add, ["Fm", "pO2"], ["LO"])
-    tt(blk(12), blk(11), blk(7), A.add, ["Fm", "pZ"], ["FZ"])
-    fill(T.onesb[:], 1.0, ["onesb"])
-    fill(T.onesf[:], 1.0, ["onesf"])
-    fill(T.cand[:], 0.0, ["cand0", "cand1"])
-    fill(T.G[:, 0:PAD], 0.0, ["Gpad"])
-    fill(T.acc[:], 0.0, ["acc0", "acc1", "acc2", "acc3", "acc4"])
-    fill(T.cb[0:1, :], 0.0, ["cb"])
-    for i in range(8):
-        ts(T.LZ[:, 16 * i:16 * i + 16], blk(12), T.NE[:, i:i + 1], A.mult, ["FZ", "NE"], ["LZ%d" % i])
-    for x in range(2):
-        ts(T.reset[:, 128 * x:128 * x + 128], T.pM[:], 0.0, A.is_equal, ["pM"], ["reset%d" % x], 1048576.0, A.mult)
-    ts(T.maskR[:], T.iM[:], col(1), A.is_equal, ["iM", "kF"], ["maskR"])
-    ts(T.posc[:], T.posb[:], pc, A.add, ["posb0", "posb16", "posb32", "posb48", "pc"], ["posc"], -0.5, A.add)
-    LZk = ["LZ%d" % i for i in range(8)]
+    cp(T.Wb[0:32, :], T.Wi[0:32, :], ["Wi"], ["Wb"])
+    cp(T.Aob[0:4, :], T.Ao[0:4, :], ["Ao"], ["Aob"])
+    dmas("stW", [("Y", T.SW[:], T.Wb[0:32, :], ["Wb"], ["SW"]), ("Y", T.LW[me], T.Wb[4 * me:4 * me + 4, :], ["Wb"], ["LWo"])])
+    iota(T.iM[:], [[1, 8], [0, 16]], 0, 0, "iM")
+    iota(T.iK[:], [[1, 32]], -1024, 0, "iK")
+    for t in range(2):
+        for ranks, h, sb, c0 in BATCH:
+            c = 32 * t + c0
+            iota(T.posb[:, c:c + 4 * len(ranks)], [[16, 4], [0, len(ranks)]], 32 + 64 * t + 1024 * h, 0, "posb%d" % c)
+    iota(T.Di[:, 0:32], [[1, 32]], -PAD, 2, "Dpad", flt=False)
+    exchange(lambda q: T.SW[q], T.LW[me], "arrW", ["SW"], "LW")
 
     for j in range(32):
         act(T.Sel[0:32, 128 * j:128 * j + 128], T.onesm[0:32, :], F.Identity, ["onesm", "Id32"], ["Sel%d" % j],
             scale=T.Id32[0:32, j:j + 1])
 
-    dmas("ldA", [("Y", T.Ai[0:32, :], T.LA[:, 0:64, :], ["LA", "LAo"], ["Ai"])])
-    dmas("ldW", [("Y", T.Wi[0:32, :], T.LA[:, 64:128, :], ["LA", "LAo"], ["Wi"])])
-    first = [me] + peers
-    dmas("ldP", [("Y", T.pinI[:, 64 * q:64 * q + 64], T.SP[q] if q == me else T.LP[q], ["SP0"] if q == me else ["LP"],
-                  ["pinI%d" % q]) for q in first])
-    dmas("ldI", [("Y", T.incI[:, 64 * q:64 * q + 64], T.SI[q] if q == me else T.LI[q], ["SI00"] if q == me else ["LI"],
-                  ["incI%d" % q]) for q in first])
-    for kh, e, sem in ((0, "Y", "ldE"), (1, "G", "ldD")):
-        dmas(sem, [(e, T.Di[32 * (q % 4) + 16 * kh:32 * (q % 4) + 16 * kh + 8, 32 + 1024 * (q // 4):1056 + 1024 * (q // 4)],
-                    T.SI[q] if q == me else T.LI[q], ["SI00" if q == me else "LI", "Dz0", "Dz1"], ["D%d%d" % (kh, q)])
-                   for q in first])
-
-    cp(T.Ab[0:32, :], T.Ai[0:32, :], ["Ai"], ["Ab"])
-    cp(T.Wb[0:32, :], T.Wi[0:32, :], ["Wi"], ["Wb"])
-    for j in range(16):
-        b = j % 8
+    def window(j, b, e, rows, r0, src, key):
         for x in range(2):
-            r = 2 * j + x
-            mm(bank(b, 256 * x, 256 * x + 256), T.Sel[0:32, 128 * r:128 * r + 128], T.Ab[0:32, :], ["Sel%d" % r, "Ab"], b)
+            r = r0 + x
+            mm(bank(b, 256 * x, 256 * x + 256), T.Sel[0:rows, 128 * r:128 * r + 128], src[0:rows, :], ["Sel%d" % r, key], b)
         out = T.win[:, 512 * j:512 * j + 512]
-        if j % 2 and j < 15:
+        if e == "V":
             ts(out, bank(b), bias, A.add, ["bias"], ["#%d" % b, "win%d" % j], 0.0, A.max)
         else:
             act(out, bank(b), F.Relu, ["bias"], ["#%d" % b, "win%d" % j], bias=bias)
+
+    ts(T.Q8[:], T.i32[:, 0:8], col(2), A.is_equal, ["i32", "kF"], ["Q8"])
+    ts(T.SelS[:], i16, col(1), A.is_equal, ["i32", "kF"], ["SelS"])
+    tt(spec, c15, c127, A.add, ["c15", "c127"], ["spec"])
+    tt(blk(1), blk(0), blk(0), A.mult, ["d"], ["d2"])
+    ts(blk(2), blk(0), 0.0, A.is_equal, ["d"], ["a0"], -2.0, A.mult)
+    ts(blk(3), i16, 0.0, A.is_equal, ["i32", "c15"], ["p0"], c15, A.mult)
+    ts(bias2, cm, 0.03125, A.mult, ["cm", "bias"], ["bias2"], bias, A.add)
+    ts(blk(5), blk(1), 1.0, A.is_equal, ["d2"], ["a1"])
+    ts(T.NE[:], T.i32[:, 0:8], col(2), A.not_equal, ["i32", "kF", "spec"], ["NE"], spec, A.max)
+    ts(blk(6), blk(3), -128.0, A.mult, ["p0"], ["pC"], c127, A.add)
+    ts(blk(7), blk(3), -112.0, A.mult, ["p0"], ["pZ"], c127, A.add)
+    ts(blk(8), blk(3), -0.5, A.mult, ["p0"], ["pO"])
+    tt(blk(9), blk(5), blk(2), A.add, ["a1", "a0"], ["F"])
+    ts(T.Idb[:], T.im[:], 0.0, A.is_equal, ["im"], ["Idb"])
+    ts(T.f[:, 144:145], T.f[:, 144:145], z0, A.add, ["F", "z0"], ["F"])
+    ts(T.t0[:], T.im[:], 0.0, A.is_gt, ["im"], ["t0"])
+    ts(T.t1[:], T.Idb[:], -1024.0, A.mult, ["Idb"], ["t1"])
+    ts(blk(11), blk(9), cm, A.mult, ["F", "cm"], ["Fm"])
+    window(2 * me, 0, "V", 4, 0, T.Aob, "Aob")
+    tt(T.LC[:], blk(11), blk(6), A.add, ["Fm", "pC"], ["LC"])
+    ts(blk(10), blk(11), 0.03125, A.mult, ["Fm"], ["Fo"])
+    tt(blk(12), blk(11), blk(7), A.add, ["Fm", "pZ"], ["FZ"])
+    tt(T.TB[:], T.t0[:], T.t1[:], A.add, ["t0", "t1"], ["TB"])
+    tt(T.LO[:], blk(10), blk(8), A.add, ["Fo", "pO"], ["LO"])
+    for i in range(8):
+        ts(T.LZ[:, 16 * i:16 * i + 16], blk(12), T.NE[:, i:i + 1], A.mult, ["FZ", "NE"], ["LZ%d" % i])
+    window(2 * me + 1, 1, "S", 4, 2, T.Aob, "Aob")
+    fill(T.onesf[:], 1.0, ["onesf"])
+    fill(lim, -992.5, ["lim"])
+    fill(T.L[:], 0, ["L0", "L1", "L2"])
+    ts(T.Id16[:], T.Idb[:], 16.0, A.mult, ["Idb"], ["Id16"])
+    fill(T.cand[:], 0.0, ["cand0", "cand1", "cand2"])
+    fill(T.G[:, 0:PAD], 0.0, ["Gpad"])
+    fill(T.acc[:], 0.0, ["acc0", "acc1", "acc2", "acc3", "acc4"])
+    fill(T.cb[0:1, :], 0.0, ["cb"])
+    for b, (ranks, h, sb, c0) in enumerate(BATCH):
+        for jj in range(4 if sb else 0):
+            fill(T.P[:, 512 * b + 128 * jj:512 * b + 128 * jj + 32 * sb], 0.0, ["Pz%d%d" % (b, jj)])
+    ts(T.reset[:], T.pM[:], 0.0, A.is_equal, ["pM"], ["reset"], 1048576.0, A.mult)
+    ts(T.pK[0:16, :], T.pM[0:16, :], 16.5, A.add, ["pM"], ["pK"], 1.0 / 512, A.mult)
+    fill(T.Di[:, 1056:DW], 0, ["Dz1"])
+    ts(T.maskR[:], T.iM[:], col(1), A.is_equal, ["iM", "kF"], ["maskR"])
+    ts(T.posc[:], T.posb[:], pc, A.add, ["posb%d" % (32 * t + b[3]) for t in range(2) for b in BATCH] + ["pc"], ["posc"],
+       0.5, A.add)
+    LZk = ["LZ%d" % i for i in range(8)]
+
+    first = [me] + peers
+    dmas("ldP", [("Y", T.pinI[:, 64 * me:64 * me + 64], T.SP[me], ["SP0"], ["pinO"])])
+    dmas("ldA", [("Y", T.Ai[0:32, :], T.LA[:], ["LA", "LAo"], ["Ai"])])
+    dmas("ldP", [("Y", T.pinI[:, 64 * q:64 * q + 64], T.LP[q], ["LP"], ["pinI%d" % n]) for n, q in enumerate(peers)])
+    dmas("stI", [("Y", T.SI[:, 16 * i:16 * i + 16, :], T.inc[:, 64 * i:64 * i + 64], [], ["SI%d" % i]) for i in range(8)])
+    exchange(lambda q: T.SI[q], T.LI[me], "arrI", ["SI0"], "LI")
+
+    def inc_of(q):
+        return (T.SI, "SI0") if q == me else (T.LI, "LI")
+
+    def load_inc(t):
+        dmas("ldI%d" % t, [("Y", T.incI[:, 256 * t + 32 * q:256 * t + 32 * q + 32], inc_of(q)[0][q, t:128:2, :], [inc_of(q)[1]],
+                            ["incI%d%d" % (t, q)]) for q in first])
+
+    def lists(t):
+        cp(T.incU[:, 256 * t:256 * t + 256], T.incI[:, 256 * t:256 * t + 256], ["incI%d0" % t], ["incU%d" % t])
+
+    cp(T.Ab[0:32, :], T.Ai[0:32, :], ["Ai"], ["Ab"])
+    for n, j in enumerate([j for j in range(16) if j // 2 != me]):
+        window(j, (n + 2) % 8, "V" if n % 2 and n < 13 else "S", 32, 2 * j, T.Ab, "Ab")
     wink = ["win%d" % j for j in range(16)]
     cp(T.pinU[:], T.pinI[:], ["pinI0"], ["pinU"])
     for t in range(2):
-        for h in range(2):
+        for ranks, h, sb, c0 in BATCH:
+            n = len(ranks)
             for jj in range(4):
-                c = 32 * t + 16 * h + 4 * jj
-                mm(bank(1, c, c + 4), T.Ab[0:32, t:256:2], T.Idb[0:32, 16 * h + jj:16 * h + 16:4], ["Ab", "Idb"], 1)
-    cp(T.own[:], bank(1, 0, 64), [], ["#1", "own"])
+                c = 32 * t + c0 + n * jj
+                mm(bank(1, c, c + n), T.Ab[0:32, t:256:2], T.Idb[0:32, 4 * ranks[0] + jj:4 * (ranks[0] + n):4], ["Ab", "Idb"], 1)
 
     for q in range(8):
         out = T.G[:, PAD + 1024 * q:PAD + 1024 * q + 1024]
@@ -282,141 +307,180 @@ def rank_program(g, core, T, topo):
             cp(out, src, wink + ["pinU"], ["G%d" % q])
         else:
             act(out, src, F.Copy, wink + ["pinU"], ["G%d" % q])
-        dmas("w%d" % q, [("Y", T.G[127:128, PAD + 1024 * q:PAD + 1024 * q + 1024], T.Wb[4 * q:4 * q + 4, :], ["Wb"], ["G%d" % q])])
+        if q == 0:
+            cp(T.own[:], bank(1, 0, 64), [], ["#1", "own"])
+            ts(T.own32[:], bank(1, 0, 64), -15.5, A.add, [], ["#1", "own32"], 0.03125, A.mult)
+        if q == 6:
+            load_inc(0)
+        dmas("w%d" % q, [("Y", T.G[127:128, PAD + 1024 * q:PAD + 1024 * q + 1024], T.LW[q], ["LW", "LWo"], ["G%d" % q])])
+    slot = {q: (h, sb + n) for ranks, h, sb, c0 in BATCH for n, q in enumerate(ranks)}
+    dmas("ldD", [("Y", T.Di[32 * slot[q][1] + 16 * kh:32 * slot[q][1] + 16 * kh + 8, 32 + 1024 * slot[q][0]:1056 + 1024 * slot[q][0]],
+                  inc_of(q)[0][q], [inc_of(q)[1], "Dz0", "Dz1"], ["D%d%d" % (kh, q)]) for q in range(8) for kh in range(2)])
+    load_inc(1)
+    dmas("ldW", [("Y", T.Wl[0:32, :], T.LW[:], ["LW", "LWo"], ["Wl"])])
     Gk = ["G%d" % q for q in range(8)]
     Zk = ["Z%d" % j for j in range(16)]
-    Dk = ["D00", "D10", "Dpad"]
-    cp(T.incU[:], T.incI[:], ["incI0"], ["incU"])
+    Dk = ["D00", "Dpad"]
+    place = {q: (b, n) for b, (ranks, h, sb, c0) in enumerate(BATCH) for n, q in enumerate(ranks)}
 
-    def gather_y(t, q, e, lo=0, hi=32):
-        out = T.Y[:, 512 * q + 16 * lo:512 * q + 16 * hi]
-        src = T.Z[:, 0:NV].indirect(T.incU[:, 64 * q + 32 * t + lo:64 * q + 32 * t + hi])
-        keys = ["Y%d%d" % (q, b) for b in range(lo // 16, hi // 16)]
-        if e == "S":
-            act(out, src, F.Copy, Zk + ["incU"], keys)
-        else:
-            cp(out, src, Zk + ["incU"], keys)
+    def key_cols(q, jj):
+        b, n = place[q]
+        c = 16 * (len(BATCH[b][0]) * jj + n)
+        return bank(b, c, c + 16)
 
-    def keys_of(t, q):
-        for jj in (0, 2, 1, 3):
-            c = 16 * (4 * jj + q % 4)
-            u = 1024 * q + 256 * jj
-            n = 512 * q + 256 * (jj & 1)
-            mm(bank(q // 4, c, c + 16), T.win[0:16, u + t:u + 256:2], T.LO[0:16, :], wink + ["LO"], q // 4, True, False)
-            mm(bank(q // 4, c, c + 16), T.Y[:, n + (jj >> 1):n + 256:2], T.SelS[:], ["Y%d%d" % (q, jj & 1), "SelS"], q // 4,
-               False, True)
+    def own_keys(t):
+        for b, (ranks, h, sb, c0) in enumerate(BATCH):
+            w = 64 * len(ranks)
+            mm(bank(b, 0, w), T.onesb[0:16, :], T.pK[0:16, 0:w], ["onesb", "pK"], b, True, False)
+            for q in ranks:
+                for jj in range(4):
+                    u = 1024 * q + 256 * jj
+                    mm(key_cols(q, jj), T.win[0:16, u + t:u + 256:2], T.LO[0:16, :], wink + ["LO"], b, False, False)
 
-    def chain(t, h):
-        H = str(h)
-        c, w = slice(16 * h, 16 * h + 16), slice(128 * h, 128 * h + 128)
-        bp, bz, bo, bv = 2 + h, 4 + h, h, 6
-        mins = T.mins[:, 256 * h:256 * h + 256]
-        op("V", ["reset0", "reset1"], ["#" + H, "mins" + H],
-           lambda: V.tensor_tensor_scan(mins, T.reset[:], bank(h, 0, 256), 0.0, A.add, A.min))
+    def gathers(t, e, pieces, left):
+        for q, xs in pieces:
+            lo, hi = 16 * xs[0], 16 * xs[-1] + 16
+            out = T.Y[:, 512 * q + 16 * lo:512 * q + 16 * hi]
+            src = T.Z[:, 0:NV].indirect(T.incU[:, 256 * t + 32 * q + lo:256 * t + 32 * q + hi])
+            keys = ["Y%d%d" % (q, x) for x in xs]
+            if e == "S":
+                act(out, src, F.Copy, Zk + ["incU%d" % t], keys)
+            else:
+                cp(out, src, Zk + ["incU%d" % t], keys)
+            b = place[q][0]
+            for x in xs:
+                n = 512 * q + 256 * x
+                for y in range(2):
+                    left[b] -= 1
+                    mm(key_cols(q, x + 2 * y), T.Y[:, n + y:n + 256:2], T.SelS[:], ["Y%d%d" % (q, x), "SelS"], b, False, left[b] == 0)
+            yield
+
+    def front(t, b):
+        ranks, h, sb, c0 = BATCH[b]
+        n = len(ranks)
+        B = str(b)
+        c, ct = slice(c0, c0 + 4 * n), slice(32 * t + c0, 32 * t + c0 + 4 * n)
+        mins = T.mins[:, 16 * c0:16 * c0 + 64 * n]
+        least = T.mins[:, 16 * c0 + 15:16 * c0 + 64 * n:16]
+        op("V", ["reset"], ["#" + B, "mins" + B],
+           lambda: V.tensor_tensor_scan(mins, T.reset[:, 0:64 * n], bank(b, 0, 64 * n), 0.0, A.add, A.min))
         yield
-        cp(T.ki[:, c], T.mins[:, 256 * h + 15:256 * h + 256:16], ["mins" + H], ["ki" + H])
+        cp(T.xi[:, c], least, ["mins" + B], ["xi" + B])
         yield
-        ts(T.ri[:, c], T.ki[:, c], 31, A.bitwise_and, ["ki" + H], ["ri" + H])
-        yield
-        ts(T.cand[:, 32 * h + 12:32 * h + 28], T.ri[:, c], 16.0, A.is_ge, ["ri" + H], ["cand" + H])
-        ts(T.rz[:, c], T.ri[:, c], 0.03125, A.mult, ["ri" + H], ["rz" + H])
+        z = 32 * b + 3 * n
+        tt(T.cand[:, z:z + 4 * n], T.xi[:, c], least, A.is_gt, ["xi" + B, "mins" + B], ["cand" + B])
         for s in range(4):
-            mm(bank(bp, 0, 16), T.TB[:] if s == 0 else T.onesb[:], T.cand[:, 32 * h + 12 - 4 * s:32 * h + 28 - 4 * s],
-               ["cand" + H, "TB", "onesb"], bp, s == 0, s == 3)
-        tt(T.zz[:, c], T.rz[:, c], T.posc[:, 32 * t + 16 * h:32 * t + 16 * h + 16], A.add, ["rz" + H, "posc"], ["zz" + H])
+            mm(bank(b, 256, 256 + 4 * n), T.TB[:] if s == 0 else T.onesb[:], T.cand[:, z - n * s:z + 4 * n - n * s],
+               ["cand" + B, "TB", "onesb"], b, s == 0, s == 3)
         yield
+        tt(T.rr[:, ct], least, T.xi[:, c], A.subtract, ["xi" + B, "mins" + B], ["rr%d%d" % (t, b)])
+        yield
+        tt(T.zz[:, c], T.rr[:, ct], T.posc[:, ct], A.add, ["rr%d%d" % (t, b), "posc"], ["zz" + B])
+        yield
+        m = 32 * (sb + n)
         for jj in range(4):
-            for q in range(4):
-                j = 4 * jj + q
-                ts(T.P[:, 512 * h + 32 * j:512 * h + 32 * j + 32], T.iK[:], bank(bp, j, j + 1), A.is_equal, ["iK", "zz" + H],
-                   ["#%d" % bp, "P%d_%d" % (h, j)], T.zz[:, 16 * h + j:16 * h + j + 1], A.mult)
-            mm(bank(bz, 0, 8), T.P[:, 512 * h + 128 * jj:512 * h + 128 * jj + 128], T.onesf[:],
-               ["P%d_%d" % (h, 4 * jj + q) for q in range(4)] + ["onesf"], bz, jj == 0, jj == 3)
-            yield
-        L = T.L[:, 8 * h:8 * h + 8]
-        ts(L, bank(bz, 0, 8), col(5), A.max, ["kF"], ["#%d" % bz, "L" + H])
-        yield
-        tt(T.XL[:, w], T.Di[:, 0:DW].indirect(L), T.maskR[:], A.mult, Dk + ["L" + H, "maskR"], ["XL" + H])
-        mm(bank(bo, 256, 264), T.XL[:, w], T.Q8[:], ["XL" + H, "Q8"], bo)
-        yield
-        fr = T.fr[:, 4 * h:4 * h + 1]
-        ts(fr, T.L[:, 8 * h:8 * h + 1], bank(bz, 0, 1), A.subtract, ["L" + H], ["#%d" % bz, "fr" + H], -32.0, A.mult)
-        act(T.E[:, w], T.Idb[:], F.Identity, ["Idb", "fr" + H], ["E" + H], scale=fr)
-        mm(bank(bv, 0, 128), T.onesm[:], T.E[:, w], ["onesm", "E" + H], bv)
-        act(T.vals[:, w], bank(bv, 0, 128), F.Relu, ["bias"], ["#%d" % bv, "vals" + H], bias=bias)
-        yield
-        off = T.off[:, 8 * h:8 * h + 8]
-        ts(off, bank(bo, 256, 264), float(PAD), A.add, [], ["#%d" % bo, "off" + H])
-        yield
-        act(T.old[:, w], T.G[:, 0:PAD + NV].indirect(off), F.Identity, Gk + ["Gpad", "off" + H, "c127"], ["old" + H], scale=c127)
-        yield
-        tt(T.G[:, 0:PAD + NV].indirect(off), T.old[:, w], T.vals[:, w], A.add, ["old" + H, "vals" + H, "off" + H], Gk + ["Gpad"])
-        yield
-
-    def third(t):
-        gather_y(t, 4, "V", 0, 16)
-        yield
-        gather_y(t, 4, "V", 16, 32)
-        yield
-        keys_of(t, 4)
-        yield
-
-    def later(t):
-        for q in (5, 6, 7):
-            keys_of(t, q)
+            p0 = 512 * b + 128 * jj
+            for x in range(n):
+                j = n * jj + x
+                p = p0 + 32 * (sb + x)
+                ts(T.P[:, p:p + 32], T.iK[:], bank(b, 256 + j, 257 + j), A.is_equal, ["iK", "zz" + B],
+                   ["#" + B, "P%d_%d" % (b, j)], T.zz[:, c0 + j:c0 + j + 1], A.mult)
+            mm(T.ps[0:m, 512 * (3 + b):512 * (3 + b) + 8], T.P[:, p0:p0 + m], T.onesf[:],
+               ["P%d_%d" % (b, n * jj + x) for x in range(n)] + ["onesf", "Pz%d%d" % (b, jj)], 3 + b, jj == 0, jj == 3)
             yield
 
-    def new_rows(t):
-        pn = T.ps[0:32, 512 * 7:512 * 7 + 128]
-        mm(pn, T.ee[:], T.Idb[:], ["ee", "Idb"], 7, True, False)
-        mm(pn, T.own[:, 32 * t:32 * t + 32], T.Idb[:], ["own", "Idb"], 7, False, True)
-        act(T.ob[0:32, t:256:2], pn, F.Copy, [], ["#7", "ob%d" % t])
+    def back(t, b):
+        ranks, h, sb, c0 = BATCH[b]
+        B = str(b)
+        lo, m = 32 * sb, 32 * (sb + len(ranks))
+        w = slice(128 * b + lo, 128 * b + m)
+        bz, bo, bv = 3 + b, 6, 7
+        ts(T.L[0:m, 8 * b:8 * b + 8], T.ps[0:m, 512 * bz:512 * bz + 8], kF[0:m, 5:6], A.max, ["kF"], ["#%d" % bz, "L" + B])
+        yield
+        fr = T.fr[0:m, 2 * b:2 * b + 1]
+        ts(fr, T.L[0:m, 8 * b:8 * b + 1], T.ps[0:m, 512 * bz:512 * bz + 1], A.subtract, ["L" + B], ["#%d" % bz, "fr" + B],
+           -32.0, A.mult)
+        act(T.E[0:m, w], T.Idb[0:m, lo:m], F.Identity, ["Idb", "fr" + B], ["E" + B], scale=fr)
+        mm(bank(bv, lo, m), T.onesm[0:m, :], T.E[0:m, w], ["onesm", "E" + B], bv)
+        yield
+        XL = T.XL[:, 128 * b:128 * b + 128]
+        tt(XL, T.Di[:, 0:DW].indirect(T.L[:, 8 * b:8 * b + 8]), T.maskR[:], A.mult, Dk + ["L" + B, "maskR"], ["XL" + B])
+        k = (m - lo) // 16
+        mm(bank(bo, 0, k), XL, T.Q8[:, lo // 16:m // 16], ["XL" + B, "Q8"], bo)
+        act(T.vals[:, w], bank(bv, lo, m), F.Relu, ["bias2"], ["#%d" % bv, "vals" + B], bias=bias2)
+        yield
+        off = T.off[:, 8 * b:8 * b + k]
+        ts(off, bank(bo, 0, k), float(PAD), A.add, [], ["#%d" % bo, "off" + B])
+        act(T.old[:, w], T.G[:, 0:PAD + NV].indirect(off), F.Identity, Gk + ["Gpad", "off" + B, "c127"], ["old" + B], scale=c127)
+        yield
+        tt(T.G[:, 0:PAD + NV].indirect(off), T.old[:, w], T.vals[:, w], A.add, ["old" + B, "vals" + B, "off" + B], Gk + ["Gpad"])
+        yield
+
+    def movers(t, b):
+        ranks, h, sb, c0 = BATCH[b]
+        act(T.le[:, 32 * t + c0:32 * t + c0 + 4 * len(ranks)], bank(b, 256, 256 + 4 * len(ranks)), F.Sign, ["lim"],
+            ["#%d" % b, "le%d%d" % (t, b)], scale=-1.0, bias=lim)
+
+    def new_parts():
+        tb = [(t, b) for t in range(2) for b in range(NB)]
+        tt(T.dd[:], T.rr[:], T.own32[:], A.subtract, ["rr%d%d" % x for x in tb] + ["own32"], ["dd"])
+        tt(T.ee[:], T.le[:], T.dd[:], A.mult, ["le%d%d" % x for x in tb] + ["dd"], ["ee"])
+        for t in range(2):
+            pn = T.ps[0:32, 512 * (4 + t):512 * (4 + t) + 128]
+            mm(pn, T.own[:, 32 * t:32 * t + 32], T.Idb[:], ["own", "Idb"], 4 + t, True, False)
+            mm(pn, T.dd[:, 32 * t:32 * t + 32], T.Id16[:], ["dd", "Id16"], 4 + t, False, False)
+            mm(pn, T.ee[:, 32 * t:32 * t + 32], T.Id16[:], ["ee", "Id16"], 4 + t, False, True)
+            act(T.ob[0:32, t:256:2], pn, F.Copy, [], ["#%d" % (4 + t), "ob%d" % t])
+        rows = [(ranks[0], len(ranks), jj, c0 + len(ranks) * jj) for ranks, h, sb, c0 in BATCH for jj in range(4)]
+        dmas("stN", [("Y", T.SN[q:q + n, 32 * jj:32 * jj + 32, :], T.ob[c:c + n, :], ["ob0", "ob1"], ["SN%d" % c])
+                     for q, n, jj, c in rows])
+        exchange(lambda q: T.SN[q], T.LN[me], "arrN", ["SN0"], "LN")
+
+    def fillers(t):
+        for b in range(NB):
+            movers(t, b)
+            yield
+        if t == 0:
+            lists(1)
+            act(T.junk[0:32, 0:256], T.Wl[0:32, :], F.Identity, ["Wl"], ["junk", "acc4"], scale=-15.0, accum_out=T.acc[0:32, 4:5])
+        else:
+            new_parts()
+        yield
 
     for t in range(2):
         for j in range(16):
             b = j % 8
             mm(bank(b), T.LZ[:], T.G[:, PAD + 512 * j:PAD + 512 * j + 512], LZk + ["G%d" % (j // 2)], b)
             out = T.Z[:, 512 * j:512 * j + 512]
-            if t == 1 and j == 2:
-                new_rows(0)
-            if j % 2 and (j < 15 or t == 1):
+            if t == 0 and j == 9:
+                lists(0)
+            if j % 2:
                 ts(out, bank(b), 0.0, A.max, [], ["#%d" % b, "Z%d" % j])
             else:
                 act(out, bank(b), F.Relu, [], ["#%d" % b, "Z%d" % j])
-        for q, e in ((0, "V"), (2, "S"), (1, "V"), (3, "S")):
-            gather_y(t, q, e, 0, 16)
-            gather_y(t, q, e, 16, 32)
-            keys_of(t, q)
-        for q in (5, 6, 7):
-            gather_y(t, q, "S")
-        if t == 0:
-            act(T.junk[0:32, :], T.Wb[0:32, :], F.Identity, ["Wb"], ["junk", "acc4"], scale=-15.0, accum_out=T.acc[0:32, 4:5])
-        steps = {"a": chain(t, 0), "b": chain(t, 1), "x": third(t), "k": later(t)}
+        own_keys(t)
+        left = [4 * len(b[0]) for b in BATCH]
+        steps = {"v": gathers(t, "V", PIECES["V"], left), "s": gathers(t, "S", PIECES["S"], left), "x": fillers(t)}
+        for b in range(NB):
+            steps["ABC"[b]], steps["abc"[b]] = front(t, b), back(t, b)
         for ch in ORDER:
-            next(steps[ch], None)
-        for h in range(2):
-            ts(T.le[:, 16 * h:16 * h + 16], bank(2 + h, 0, 16), 1055.5, A.is_le, [], ["#%d" % (2 + h), "le%d" % h])
-        ts(T.bi[:], T.ki[:], 15, A.bitwise_and, ["ki0", "ki1"], ["bi"])
-        tt(T.dd[:], T.bi[:], T.own[:, 32 * t:32 * t + 32], A.subtract, ["bi", "own"], ["dd"])
-        tt(T.ee[:], T.le[:], T.dd[:], A.mult, ["le0", "le1", "dd"], ["ee"])
+            next(steps[ch])
+        for ch in steps:
+            assert next(steps[ch], 1) == 1, ch
 
-    for r in range(4):
-        for x in range(16):
-            e0 = PAD + 128 * (16 * r + x)
+    e0 = PAD
+    for r, n in enumerate(CUT):
+        for x in range(n):
             mm(bank(r, 16 * x, 16 * x + 16), T.G[:, e0:e0 + 128], T.LC[:], Gk + ["LC"], r)
-        act(T.junk[:], bank(r, 0, 256), F.Relu, [], ["#%d" % r, "junk", "acc%d" % r], accum_out=T.acc[:, r:r + 1])
-        if r == 0:
-            new_rows(1)
-            dmas("stN", [("Y", T.SN[4 * h:4 * h + 4, 32 * jj:32 * jj + 32, :], T.ob[16 * h + 4 * jj:16 * h + 4 * jj + 4, :],
-                          ["ob0", "ob1"], ["SN%d%d" % (h, jj)]) for h in range(2) for jj in range(4)])
-            exchange(lambda q: T.SN[q], T.LN[me], "arrN", ["SN00"], "LN")
+            e0 += 128
+        act(T.junk[:, 0:16 * n], bank(r, 0, 16 * n), F.Relu, [], ["#%d" % r, "junk", "acc%d" % r], accum_out=T.acc[:, r:r + 1])
     pcut = T.ps[0:1, 512 * 6:512 * 6 + 8]
     mm(pcut, T.onesf[:, 0:1], T.acc[:], ["onesf", "acc0", "acc1", "acc2", "acc3", "acc4"], 6)
     op("V", [], ["#6", "cb"], lambda: V.tensor_reduce(T.cb[0:1, 0:1], pcut, AxisListType.X, A.add, negate=True))
     dmas("stU", [("S", T.SU[:], T.cb[0:1, :], ["cb"], ["SU"])])
     exchange(lambda q: T.SU[:], T.LU[me], "arrU", ["SU"], "LU")
 
-    outs = [("Y", T.newpart[me:me + 1, :], T.SN[me], ["SN00"], ["o0"])]
+    outs = [("Y", T.newpart[me:me + 1, :], T.SN[me], ["SN0"], ["o0"])]
     if me > 0:
         outs.append(("Y", T.newpart[0:me, :], T.LN[0:me], ["LN"], ["o1"]))
     if me < N - 1:

@@ -3,51 +3,55 @@ from concourse.mybir import AluOpType, AxisListType, ActivationFunctionType
 
 PAD = 288
 NV = 8192
-DW = 32 + 2048
-BATCH = (((0, 1, 2, 3), 0, 0, 0), ((4, 5, 6, 7), 1, 0, 16))
-ORDER = "vsvsvsv" "AsvAAAAssAAsAAx" "BBaBBaBaBBBBxabbbabxb"
-PIECES = {"V": ((0, (0, 1)), (2, (0,)), (2, (1,)), (4, (0,)), (4, (1,))),
-          "S": ((1, (0, 1)), (3, (0,)), (3, (1,)), (5, (0, 1)), (6, (0, 1)), (7, (0,)), (7, (1,)))}
-CUT = (20, 20, 16, 8)
+KW = 19
+POS = 320
+DW = 32 + 1024
+BATCH = (((0, 1, 2, 3), 0, 0, 0), ((4, 5), 1, 2, 16), ((6, 7), 1, 0, 24))
+ORDER = "vsvsvsvAAAssAABABBAssBBBsaxBaaCbCxCbabCCCCacbccxxbcxc"
+PIECES = {"V": ((0, (0, 1)), (2, (0,)), (2, (1,)), (4, (0,))),
+          "S": ((1, (0, 1)), (3, (0,)), (3, (1,)), (4, (1,)), (5, (0, 1)), (6, (0, 1)), (7, (0,)), (7, (1,)))}
+SHIFT = 192
+SEL = 22
+CUT = (16, 16, 12, 10, 6, 4)
 
 SCRATCH = {
-    "SA": ("dram", [8, 128, 8], "int32"), "LA": ("dram", [8, 128, 8], "int32"),
+    "SA": ("dram", [4, 128, 16], "int32"), "LA": ("dram", [8, 128, 16], "int32"),
     "SW": ("dram", [8, 128, 8], "bfloat16"), "LW": ("dram", [8, 128, 8], "bfloat16"),
-    "SP": ("dram", [8, 128, 64], "int32"), "LP": ("dram", [8, 128, 64], "int32"),
+    "SP": ("dram", [8, 128, 64], "uint16"), "LP": ("dram", [8, 128, 64], "uint16"),
     "SI": ("dram", [8, 128, 64], "int32"), "LI": ("dram", [8, 128, 64], "int32"),
     "SN": ("dram", [8, 128, 8], "float32"), "LN": ("dram", [8, 128, 8], "float32"),
-    "SU": ("dram", [128, 2], "float32"), "LU": ("dram", [8, 128, 2], "float32"),
     "win": ("sbuf", [128, NV], "bfloat16"), "G": ("sbuf", [128, PAD + NV], "bfloat16"),
     "Z": ("sbuf", [128, NV], "bfloat16"), "Y": ("sbuf", [128, 4096], "bfloat16"),
-    "Di": ("sbuf", [128, DW], "int32"), "P": ("sbuf", [128, 1536], "float32"),
+    "Di": ("sbuf", [128, 2 * DW], "int32"), "P": ("sbuf", [128, 12, 128], "float32"),
     "pinI": ("sbuf", [128, 512], "int32"), "incI": ("sbuf", [128, 512], "int32"),
-    "pinU": ("sbuf", [128, 512], "uint16"), "incU": ("sbuf", [128, 512], "uint16"),
+    "pinS": ("sbuf", [128, 512], "uint16"), "pinU": ("sbuf", [128, 512], "uint16"), "incU": ("sbuf", [128, 512], "uint16"),
     "Ai": ("sbuf", [128, 256], "int32"), "Wi": ("sbuf", [128, 256], "int32"), "Ao": ("sbuf", [128, 256], "int32"),
     "Ab": ("sbuf", [128, 256], "bfloat16"), "Wb": ("sbuf", [128, 256], "bfloat16"), "Aob": ("sbuf", [128, 256], "bfloat16"),
-    "Wl": ("sbuf", [128, 256], "bfloat16"), "junk": ("sbuf", [128, 320], "bfloat16"),
-    "Sel": ("sbuf", [128, 4096], "bfloat16"), "reset": ("sbuf", [128, 256], "float32"), "pK": ("sbuf", [128, 256], "bfloat16"),
-    "kI": ("sbuf", [128, 8], "int32"), "kF": ("sbuf", [128, 32], "float32"),
-    "im": ("sbuf", [128, 128], "float32"), "iM": ("sbuf", [128, 128], "float32"), "pM": ("sbuf", [128, 256], "float32"),
-    "i32": ("sbuf", [128, 32], "float32"), "iK": ("sbuf", [128, 32], "float32"), "posc": ("sbuf", [128, 64], "float32"),
+    "Wl": ("sbuf", [128, 256], "bfloat16"), "junk": ("sbuf", [128, 1536], "bfloat16"),
+    "Sel": ("sbuf", [128, 4096], "bfloat16"), "reset": ("sbuf", [128, 32 * KW], "float32"),
+    "pK": ("sbuf", [128, 16 * KW], "bfloat16"), "onesk": ("sbuf", [128, 128], "bfloat16"),
+    "kI": ("sbuf", [128, 8], "int32"), "kF": ("sbuf", [128, 32], "float32"), "iM": ("sbuf", [128, 128], "float32"),
+    "i32": ("sbuf", [128, 32], "float32"), "iK": ("sbuf", [128, 32], "float32"), "posc": ("sbuf", [128, 2, 32], "float32"),
     "posb": ("sbuf", [128, 64], "float32"),
     "Idb": ("sbuf", [128, 128], "bfloat16"), "Id32": ("sbuf", [128, 32], "float32"), "TB": ("sbuf", [128, 128], "bfloat16"),
-    "t0": ("sbuf", [128, 128], "bfloat16"), "t1": ("sbuf", [128, 128], "bfloat16"),
+    "t0": ("sbuf", [128, 128], "bfloat16"), "Ib": ("sbuf", [128, 32], "bfloat16"),
     "onesb": ("sbuf", [128, 128], "bfloat16"), "onesm": ("sbuf", [128, 128], "bfloat16"), "onesf": ("sbuf", [128, 8], "float32"),
     "maskR": ("sbuf", [128, 128], "float32"), "Q8": ("sbuf", [128, 8], "float32"), "NE": ("sbuf", [128, 8], "float32"),
     "SelS": ("sbuf", [128, 16], "bfloat16"), "LZ": ("sbuf", [128, 128], "bfloat16"),
     "LC": ("sbuf", [128, 16], "bfloat16"), "LO": ("sbuf", [128, 16], "bfloat16"), "f": ("sbuf", [128, 256], "float32"),
-    "own": ("sbuf", [128, 64], "bfloat16"), "own32": ("sbuf", [128, 64], "float32"), "mins": ("sbuf", [128, 512], "float32"),
-    "xi": ("sbuf", [128, 32], "int32"), "cand": ("sbuf", [128, 96], "bfloat16"), "rr": ("sbuf", [128, 64], "float32"),
-    "zz": ("sbuf", [128, 32], "float32"), "dd": ("sbuf", [128, 64], "bfloat16"), "le": ("sbuf", [128, 64], "float32"),
-    "ee": ("sbuf", [128, 64], "bfloat16"), "Id16": ("sbuf", [128, 128], "bfloat16"),
+    "own": ("sbuf", [128, 64], "bfloat16"), "own32": ("sbuf", [128, 64], "float32"), "mins": ("sbuf", [128, 32 * KW], "float32"),
+    "cand": ("sbuf", [128, 8, 8], "bfloat16"), "ownp": ("sbuf", [128, 64], "float32"),
+    "zz": ("sbuf", [128, 64], "float32"), "dd": ("sbuf", [128, 64], "bfloat16"), "le": ("sbuf", [128, 64], "float32"),
+    "ee": ("sbuf", [128, 64], "bfloat16"),
     "L": ("sbuf", [128, 24], "uint16"), "XL": ("sbuf", [128, 384], "float32"), "fr": ("sbuf", [128, 8], "float32"),
     "E": ("sbuf", [128, 384], "bfloat16"), "off": ("sbuf", [128, 24], "uint16"),
     "vals": ("sbuf", [128, 384], "bfloat16"), "old": ("sbuf", [128, 384], "bfloat16"),
-    "ob": ("sbuf", [128, 256], "float32"), "acc": ("sbuf", [128, 8], "float32"), "cb": ("sbuf", [128, 256], "float32"),
+    "ob": ("sbuf", [128, 256], "float32"), "acc": ("sbuf", [128, 8], "float32"), "cb": ("sbuf", [128, 8], "float32"),
+    "CU": ("sbuf", [128, 8], "float32"),
     "ps": ("psum", [128, 4096], "float32"),
 }
 SEMAPHORES = (["cV", "cS", "cT", "cG", "stA", "stP", "stI", "stW", "ownA", "arrA", "arrP", "arrW", "arrI", "arrN", "arrU", "sent",
-               "ldO", "ldV", "ldA", "ldW", "ldP", "ldI0", "ldI1", "ldD", "stN", "stU", "outN", "outU"]
+               "ldO", "ldN", "ldV", "ldA", "ldW", "ldP", "ldI0", "ldI1", "ldD", "stN", "outN", "outU"]
               + ["w%d" % q for q in range(8)])
 
 A = AluOpType
@@ -106,24 +110,28 @@ def rank_program(g, core, T, topo):
             done(("dma", sem, end), rd, wr)
 
     peers = [(me + d) % N for d in range(1, N)]
-    eng, used = {}, []
-    for q in sorted(peers, key=lambda q: len(topo.engines(core, cores[q]))):
-        free = [x for x in topo.engines(core, cores[q]) if x not in used]
-        pick = free[0] if topo.chip(core) != topo.chip(cores[q]) else free[-1]
-        eng[q] = pick
-        used.append(pick)
+    near = [q for q in peers if topo.chip(cores[q]) == topo.chip(core)]
+    far = [q for q in peers if q not in near]
+    far_eng = topo.engines(core, cores[far[0]])
+    near_eng = [x for x in topo.engines(core, cores[near[0]]) if x not in far_eng]
+    chips = sorted(set(topo.chip(c) for c in cores))
+    on_chip = [[q for q in range(N) if topo.chip(cores[q]) == c] for c in chips]
 
-    def exchange(src_of, dst, arr, rd, landed):
+    def send(transfers, dst, arr, rd, landed):
         order("G", rd, [])
         trs = []
-        for q in peers:
-            rid, pid, _ = topo.addr(cores[q])
-            trs.append(RemoteDMATransfer(dst_ids=[DstId(rid=rid, pnc=pid)], dma_engine_mask=1 << eng[q],
-                                         remote_sem=T.sem[arr], src=src_of(q), dst=dst))
+        for ranks, src, engines in transfers:
+            ids = [DstId(rid=topo.addr(cores[q])[0], pnc=topo.addr(cores[q])[1]) for q in ranks]
+            trs.append(RemoteDMATransfer(dst_ids=ids, dma_engine_mask=sum(1 << x for x in engines), remote_sem=T.sem[arr],
+                                         srcs=[src], dsts=[dst] * len(ranks)))
         g.remote_dma_fused(trs, local_sem=T.sem.sent)
-        total["sent"] = total.get("sent", 0) + len(peers)
-        total[arr] = len(peers)
-        wrote[landed] = ("far", arr, len(peers))
+        total["sent"] = total.get("sent", 0) + sum(len(x[2]) for x in transfers)
+        total[arr] = sum(len(x[0]) * len(x[2]) for x in transfers)
+        wrote[landed] = ("far", arr, total[arr])
+
+    def exchange(src_of, dst, arr, rd, landed, last=False):
+        fe, ne = (far_eng[-len(far):], near_eng[-len(near):]) if last else (far_eng, near_eng)
+        send([([q], src_of(q), [x]) for q, x in list(zip(far, fe)) + list(zip(near, ne))], dst, arr, rd, landed)
 
     V, S, PE = g.vector, g.scalar, g.tensor
 
@@ -154,22 +162,25 @@ def rank_program(g, core, T, topo):
         else:
             op("G", [], [key], lambda: g.iota(out, pattern, base, cm))
 
+    def select(out, in_, cmp, x, rd, key):
+        op("G", rd, [key], lambda: g.affine_select(out, in_, [[1, 128]], cmp, x, 0, -1))
+
     def bank(b, lo=0, hi=512):
         return T.ps[:, 512 * b + lo:512 * b + hi]
 
     dmas("stA", [("Y", T.SA[:], T.part[:], [], ["SA"])])
-    dmas("ldO", [("Y", T.Ao[0:4, :], T.part[me:me + 1, :], [], ["Ao"])])
+    dmas("ldO", [("S", T.Ao[0:4, :], T.part[me:me + 1, :], [], ["Ao"])])
+    dmas("ldN", [("Y", T.pinI[:], T.pin[:], [], ["pinI"])])
     dmas("ldV", [("S", T.Wi[0:32, :], T.w[:], [], ["Wi"])])
-    dmas("ownA", [("S", T.LA[me], T.part[me:me + 1, :], [], ["LAo"])])
-    dmas("stP", [("Y" if i % 2 else "S", T.SP[:, 16 * i:16 * i + 16, :], T.pin[:, 64 * i:64 * i + 64], [], ["SP%d" % i])
-                 for i in range(8)])
+    mine = chips.index(topo.chip(core))
+    rows = slice(64 * on_chip[mine].index(me), 64 * on_chip[mine].index(me) + 64)
+    dmas("ownA", [("S", T.LA[me, rows, :], T.part[me:me + 1, :], [], ["LAo"])])
 
     iota(T.kI[:, 0:1], [[0, 1]], 0, 1, "k", flt=False)
     iota(T.i32[:], [[1, 32]], 0, 0, "i32")
-    iota(T.pM[:], [[0, 16], [1, 16]], 0, 0, "pM")
-    iota(T.im[:], [[1, 128]], 0, -1, "im")
-    exchange(lambda q: T.SA[q], T.LA[me], "arrA", ["SA"], "LA")
-    exchange(lambda q: T.SP[q], T.LP[me], "arrP", ["SP0"], "LP")
+    others = [k for k in range(len(chips)) if me not in on_chip[k]]
+    send([(on_chip[k], T.SA[k], [far_eng[2 * n]]) for n, k in enumerate(others)] + [(near, T.SA[mine], near_eng[:1])],
+         T.LA[me], "arrA", ["SA"], "LA")
 
     kF = T.kF
     i16 = T.i32[:, 0:16]
@@ -180,17 +191,20 @@ def rank_program(g, core, T, topo):
     def blk(j):
         return T.f[:, 16 * j:16 * j + 16]
 
-    fill(T.Di[:, 32:1056], 0, ["Dz0"])
+    c15, c127, z0, cm, pc, b0, spec, bias, bias2, lim = [col(j) for j in range(8, 18)]
+    fill(T.onesb[:], 1.0, ["onesb"])
+    fill(T.onesm[:], 1.0, ["onesm"])
+    fill(T.onesk[0:16, :], 2.0 ** -10, ["onesk"])
+    fill(T.onesm[:, 15:128:16], 0.0, ["onesm"])
     ts(T.kI[:, 1:2], T.kI[:, 0:1], 15, A.bitwise_and, ["k"], ["k1"])
     ts(T.kI[:, 2:3], T.kI[:, 0:1], 4, A.arith_shift_right, ["k"], ["k2"])
     ts(T.kI[:, 3:4], T.kI[:, 0:1], 7, A.bitwise_and, ["k"], ["k3"])
     ts(T.kI[:, 4:5], T.kI[:, 0:1], 3, A.arith_shift_right, ["k"], ["k4"])
     ts(T.kI[:, 5:6], T.kI[:, 0:1], 31, A.bitwise_and, ["k"], ["k5"])
-    ts(T.onesm[:], T.pM[:, 0:128], 15.0, A.not_equal, ["pM"], ["onesm"])
+    fill(T.L[:], 0, ["L0", "L1", "L2"])
     cp(kF[:, 0:6], T.kI[:, 0:6], ["k", "k1", "k2", "k3", "k4", "k5"], ["kF"])
-    fill(T.onesb[:], 1.0, ["onesb"])
+    fill(lim, -992.5, ["lim"])
     ts(T.Id32[:], T.i32[:], col(0), A.is_equal, ["i32", "kF"], ["Id32"])
-    c15, c127, z0, cm, pc, b0, spec, bias, bias2, lim = [col(j) for j in range(8, 18)]
     ts(c15, col(0), 15.0, A.is_equal, ["kF"], ["c15"])
     ts(cm, col(1), 15.0, A.not_equal, ["kF"], ["cm"], -16.0, A.mult)
     ts(c127, col(0), 127.0, A.is_equal, ["kF"], ["c127"])
@@ -199,84 +213,92 @@ def rank_program(g, core, T, topo):
     ts(pc, col(3), 128.0, A.mult, ["kF"], ["pc"], col(4), A.add)
     ts(blk(0), i16, col(1), A.subtract, ["i32", "kF"], ["d"])
     tt(bias, b0, c15, A.add, ["b0", "c15"], ["bias"])
-    cp(T.Wb[0:32, :], T.Wi[0:32, :], ["Wi"], ["Wb"])
-    cp(T.Aob[0:4, :], T.Ao[0:4, :], ["Ao"], ["Aob"])
-    dmas("stW", [("Y", T.SW[:], T.Wb[0:32, :], ["Wb"], ["SW"]), ("Y", T.LW[me], T.Wb[4 * me:4 * me + 4, :], ["Wb"], ["LWo"])])
-    iota(T.iM[:], [[1, 8], [0, 16]], 0, 0, "iM")
-    iota(T.iK[:], [[1, 32]], -1024, 0, "iK")
-    for t in range(2):
-        for ranks, h, sb, c0 in BATCH:
-            c = 32 * t + c0
-            iota(T.posb[:, c:c + 4 * len(ranks)], [[16, 4], [0, len(ranks)]], 32 + 64 * t + 1024 * h, 0, "posb%d" % c)
-    iota(T.Di[:, 0:32], [[1, 32]], -PAD, 2, "Dpad", flt=False)
-    exchange(lambda q: T.SW[q], T.LW[me], "arrW", ["SW"], "LW")
-
-    for j in range(32):
-        act(T.Sel[0:32, 128 * j:128 * j + 128], T.onesm[0:32, :], F.Identity, ["onesm", "Id32"], ["Sel%d" % j],
-            scale=T.Id32[0:32, j:j + 1])
-
-    def window(j, b, e, rows, r0, src, key):
-        for x in range(2):
-            r = r0 + x
-            mm(bank(b, 256 * x, 256 * x + 256), T.Sel[0:rows, 128 * r:128 * r + 128], src[0:rows, :], ["Sel%d" % r, key], b)
-        out = T.win[:, 512 * j:512 * j + 512]
-        if e == "V":
-            ts(out, bank(b), bias, A.add, ["bias"], ["#%d" % b, "win%d" % j], 0.0, A.max)
-        else:
-            act(out, bank(b), F.Relu, ["bias"], ["#%d" % b, "win%d" % j], bias=bias)
-
     ts(T.Q8[:], T.i32[:, 0:8], col(2), A.is_equal, ["i32", "kF"], ["Q8"])
     ts(T.SelS[:], i16, col(1), A.is_equal, ["i32", "kF"], ["SelS"])
     tt(spec, c15, c127, A.add, ["c15", "c127"], ["spec"])
     tt(blk(1), blk(0), blk(0), A.mult, ["d"], ["d2"])
     ts(blk(2), blk(0), 0.0, A.is_equal, ["d"], ["a0"], -2.0, A.mult)
     ts(blk(3), i16, 0.0, A.is_equal, ["i32", "c15"], ["p0"], c15, A.mult)
-    ts(bias2, cm, 0.03125, A.mult, ["cm", "bias"], ["bias2"], bias, A.add)
+    cp(T.Aob[0:4, :], T.Ao[0:4, :], ["Ao"], ["Aob"])
+    cp(T.pinS[:], T.pinI[:], ["pinI"], ["pinS"])
+    dmas("stP", [("Y", T.SP[:, 16 * i:16 * i + 16, :], T.pinS[:, 64 * i:64 * i + 64], ["pinS"], ["SP%d" % i]) for i in range(8)])
+    iota(T.posb[:], [[64, 2], [0, 8], [16, 4]], 32, 0, "posb")
+    iota(T.iM[:], [[1, 8], [0, 16]], 0, 0, "iM")
+    select(T.Idb[:], T.onesb[:], A.is_equal, 0.0, ["onesb"], "Idb")
+    exchange(lambda q: T.SP[q], T.LP[me], "arrP", ["SP0"], "LP")
+    cp(T.Wb[0:32, :], T.Wi[0:32, :], ["Wi"], ["Wb"])
+    dmas("stW", [("Y", T.SW[:], T.Wb[0:32, :], ["Wb"], ["SW"]), ("Y", T.LW[me], T.Wb[4 * me:4 * me + 4, :], ["Wb"], ["LWo"])])
+
+    for h in range(2):
+        iota(T.Di[:, DW * h:DW * h + 32], [[1, 32]], -PAD, 2, "Dpad%d" % h, flt=False)
+        iota(T.Di[:, DW * h + 32:DW * h + DW], [[0, 1024]], 0, 0, "Dz%d" % h, flt=False)
+        if h == 0:
+            exchange(lambda q: T.SW[q], T.LW[me], "arrW", ["SW"], "LW", last=True)
+    select(T.t0[:], T.onesb[:], A.is_gt, 0.0, ["onesb"], "t0")
+    iota(T.iK[:], [[1, 32]], -1024, 0, "iK")
+    select(T.TB[:], T.t0[:], A.not_equal, -1024.0, ["t0"], "TB")
+
+    for j in range(SEL):
+        act(T.Sel[0:32, 128 * j:128 * j + 128], T.onesm[0:32, :], F.Identity, ["onesm", "Id32"], ["Sel%d" % j],
+            scale=T.Id32[0:32, j:j + 1])
+
+    def window(j, b, e, rows, r, src, key):
+        mm(bank(b, 0, 256), T.Sel[0:rows, 128 * r:128 * r + 128], src[0:rows, :], ["Sel%d" % r, key], b)
+        out = T.win[:, 256 * j:256 * j + 256]
+        if e == "V":
+            ts(out, bank(b, 0, 256), bias, A.add, ["bias"], ["#%d" % b, "win%d" % j], 0.0, A.max)
+        else:
+            act(out, bank(b, 0, 256), F.Relu, ["bias"], ["#%d" % b, "win%d" % j], bias=bias)
+
+    ts(bias2, cm, -0.96875, A.mult, ["cm", "bias"], ["bias2"], bias, A.add)
     ts(blk(5), blk(1), 1.0, A.is_equal, ["d2"], ["a1"])
     ts(T.NE[:], T.i32[:, 0:8], col(2), A.not_equal, ["i32", "kF", "spec"], ["NE"], spec, A.max)
     ts(blk(6), blk(3), -128.0, A.mult, ["p0"], ["pC"], c127, A.add)
     ts(blk(7), blk(3), -112.0, A.mult, ["p0"], ["pZ"], c127, A.add)
     ts(blk(8), blk(3), -0.5, A.mult, ["p0"], ["pO"])
     tt(blk(9), blk(5), blk(2), A.add, ["a1", "a0"], ["F"])
-    ts(T.Idb[:], T.im[:], 0.0, A.is_equal, ["im"], ["Idb"])
+    cp(T.Ib[0:32, :], T.Id32[0:32, :], ["Id32"], ["Ib"])
     ts(T.f[:, 144:145], T.f[:, 144:145], z0, A.add, ["F", "z0"], ["F"])
-    ts(T.t0[:], T.im[:], 0.0, A.is_gt, ["im"], ["t0"])
-    ts(T.t1[:], T.Idb[:], -1024.0, A.mult, ["Idb"], ["t1"])
+    for j in range(SEL, 32):
+        ts(T.Sel[0:32, 128 * j:128 * j + 128], T.onesm[0:32, :], T.Ib[0:32, j:j + 1], A.mult, ["onesm", "Ib"], ["Sel%d" % j])
     ts(blk(11), blk(9), cm, A.mult, ["F", "cm"], ["Fm"])
-    window(2 * me, 0, "V", 4, 0, T.Aob, "Aob")
+    for r in range(2):
+        window(4 * me + r, r, "V", 4, r, T.Aob, "Aob")
     tt(T.LC[:], blk(11), blk(6), A.add, ["Fm", "pC"], ["LC"])
     ts(blk(10), blk(11), 0.03125, A.mult, ["Fm"], ["Fo"])
     tt(blk(12), blk(11), blk(7), A.add, ["Fm", "pZ"], ["FZ"])
-    tt(T.TB[:], T.t0[:], T.t1[:], A.add, ["t0", "t1"], ["TB"])
     tt(T.LO[:], blk(10), blk(8), A.add, ["Fo", "pO"], ["LO"])
+    for r in range(2, 4):
+        window(4 * me + r, r, "S", 4, r, T.Aob, "Aob")
     for i in range(8):
-        ts(T.LZ[:, 16 * i:16 * i + 16], blk(12), T.NE[:, i:i + 1], A.mult, ["FZ", "NE"], ["LZ%d" % i])
-    window(2 * me + 1, 1, "S", 4, 2, T.Aob, "Aob")
-    fill(T.onesf[:], 1.0, ["onesf"])
-    fill(lim, -992.5, ["lim"])
-    fill(T.L[:], 0, ["L0", "L1", "L2"])
-    ts(T.Id16[:], T.Idb[:], 16.0, A.mult, ["Idb"], ["Id16"])
-    fill(T.cand[:], 0.0, ["cand0", "cand1", "cand2"])
-    fill(T.G[:, 0:PAD], 0.0, ["Gpad"])
-    fill(T.acc[:], 0.0, ["acc0", "acc1", "acc2", "acc3", "acc4"])
-    fill(T.cb[0:1, :], 0.0, ["cb"])
-    for b, (ranks, h, sb, c0) in enumerate(BATCH):
-        for jj in range(4 if sb else 0):
-            fill(T.P[:, 512 * b + 128 * jj:512 * b + 128 * jj + 32 * sb], 0.0, ["Pz%d%d" % (b, jj)])
-    ts(T.reset[:], T.pM[:], 0.0, A.is_equal, ["pM"], ["reset"], 1048576.0, A.mult)
-    ts(T.pK[0:16, :], T.pM[0:16, :], 16.5, A.add, ["pM"], ["pK"], 1.0 / 512, A.mult)
-    fill(T.Di[:, 1056:DW], 0, ["Dz1"])
+        act(T.LZ[:, 16 * i:16 * i + 16], blk(12), F.Identity, ["FZ", "NE"], ["LZ%d" % i], scale=T.NE[:, i:i + 1])
+    ts(T.posc[:], T.posb[:], pc, A.add, ["posb", "pc"], ["posc"])
     ts(T.maskR[:], T.iM[:], col(1), A.is_equal, ["iM", "kF"], ["maskR"])
-    ts(T.posc[:], T.posb[:], pc, A.add, ["posb%d" % (32 * t + b[3]) for t in range(2) for b in BATCH] + ["pc"], ["posc"],
-       0.5, A.add)
     LZk = ["LZ%d" % i for i in range(8)]
 
     first = [me] + peers
-    dmas("ldP", [("Y", T.pinI[:, 64 * me:64 * me + 64], T.SP[me], ["SP0"], ["pinO"])])
-    dmas("ldA", [("Y", T.Ai[0:32, :], T.LA[:], ["LA", "LAo"], ["Ai"])])
-    dmas("ldP", [("Y", T.pinI[:, 64 * q:64 * q + 64], T.LP[q], ["LP"], ["pinI%d" % n]) for n, q in enumerate(peers)])
-    dmas("stI", [("Y", T.SI[:, 16 * i:16 * i + 16, :], T.inc[:, 64 * i:64 * i + 64], [], ["SI%d" % i]) for i in range(8)])
+    dmas("ldA", [("Y", T.Ai[0:32, :], T.LA[:, rows, :], ["LA", "LAo"], ["Ai"])])
+    dmas("ldP", [("Y", T.pinU[:, 64 * q:64 * q + 64], T.SP[q] if q == me else T.LP[q], ["SP0" if q == me else "LP"], ["pinU%d" % q])
+                 for q in first])
+    dmas("stI", [("Y", T.SI[:, 16 * i:16 * i + 16, :], T.inc[:, 64 * i:64 * i + 64], ["LP"], ["SI%d" % i]) for i in range(8)])
     exchange(lambda q: T.SI[q], T.LI[me], "arrI", ["SI0"], "LI")
+    iota(T.reset[:], [[0, 32 * KW]], 0, 0, "reset")
+    for c, x in ((0, 1 << 20), (16, -3 << 22), (17, 3 << 22)):
+        iota(T.reset[:, c:32 * KW:KW], [[0, 32]], x, 0, "reset")
+    iota(T.pK[0:16, :], [[0, 16], [2, KW]], 33, 0, "pK")
+    for c in (17, 18):
+        iota(T.pK[0:16, c:16 * KW:KW], [[0, 16]], 8192, 0, "pK")
+    iota(T.cand[:], [[0, 64]], 0, 0, "cand")
+    iota(T.onesf[:], [[0, 8]], 1, 0, "onesf")
+    for b, (ranks, h, sb, c0) in enumerate(BATCH):
+        if sb:
+            iota(T.P[:, 4 * b:4 * b + 4, 0:32 * sb], [[0, 128 * sb]], 0, 0, "Pz%d" % b)
+    iota(T.G[:, 0:PAD], [[0, PAD]], 0, 0, "Gpad")
+    iota(T.acc[:], [[0, 8]], 0, 0, "acc7")
+    iota(T.cb[:], [[0, 8]], 0, 0, "cb")
+    acck = ["acc%d" % r for r in range(8)]
+    for k in acck:
+        wrote[k] = wrote["acc7"]
 
     def inc_of(q):
         return (T.SI, "SI0") if q == me else (T.LI, "LI")
@@ -289,49 +311,51 @@ def rank_program(g, core, T, topo):
         cp(T.incU[:, 256 * t:256 * t + 256], T.incI[:, 256 * t:256 * t + 256], ["incI%d0" % t], ["incU%d" % t])
 
     cp(T.Ab[0:32, :], T.Ai[0:32, :], ["Ai"], ["Ab"])
-    for n, j in enumerate([j for j in range(16) if j // 2 != me]):
-        window(j, (n + 2) % 8, "V" if n % 2 and n < 13 else "S", 32, 2 * j, T.Ab, "Ab")
-    wink = ["win%d" % j for j in range(16)]
-    cp(T.pinU[:], T.pinI[:], ["pinI0"], ["pinU"])
+    for n, j in enumerate([j for j in range(32) if j // 4 != me]):
+        window(j, (n + 4) % 8, "V" if n % 2 else "S", 32, j, T.Ab, "Ab")
+    wink = ["win%d" % j for j in range(32)]
     for t in range(2):
-        for ranks, h, sb, c0 in BATCH:
-            n = len(ranks)
-            for jj in range(4):
-                c = 32 * t + c0 + n * jj
-                mm(bank(1, c, c + n), T.Ab[0:32, t:256:2], T.Idb[0:32, 4 * ranks[0] + jj:4 * (ranks[0] + n):4], ["Ab", "Idb"], 1)
+        mm(bank(1, 32 * t, 32 * t + 32), T.Ab[0:32, t:256:2], T.Idb[0:32, 0:32], ["Ab", "Idb"], 1)
 
+    ends = [1024 * q for q in range(7)] + [7168 - SHIFT, NV]
     for q in range(8):
-        out = T.G[:, PAD + 1024 * q:PAD + 1024 * q + 1024]
-        src = T.win[:, 0:NV].indirect(T.pinU[:, 64 * q:64 * q + 64])
+        lo, hi = ends[q], ends[q + 1]
+        out = T.G[:, PAD + lo:PAD + hi]
+        src = T.win[:, 0:NV].indirect(T.pinU[:, lo // 16:hi // 16])
         if q % 2 == 0:
-            cp(out, src, wink + ["pinU"], ["G%d" % q])
+            cp(out, src, wink + ["pinU0", "LP"], ["g%d" % q])
         else:
-            act(out, src, F.Copy, wink + ["pinU"], ["G%d" % q])
+            act(out, src, F.Copy, wink + ["pinU0", "LP"], ["g%d" % q])
         if q == 0:
-            cp(T.own[:], bank(1, 0, 64), [], ["#1", "own"])
+            ts(T.own[:], bank(1, 0, 64), 0.0625, A.mult, [], ["#1", "own"])
             ts(T.own32[:], bank(1, 0, 64), -15.5, A.add, [], ["#1", "own32"], 0.03125, A.mult)
+        if q == 2:
+            tt(T.ownp[:], T.own32[:], T.posc[:], A.add, ["own32", "posc"], ["ownp"])
         if q == 6:
+            ts(T.reset[:, 18:32 * KW:KW], T.posc[:, :, 0:16], -1.0, A.mult, ["posc"], ["reset"])
             load_inc(0)
-        dmas("w%d" % q, [("Y", T.G[127:128, PAD + 1024 * q:PAD + 1024 * q + 1024], T.LW[q], ["LW", "LWo"], ["G%d" % q])])
+        for x in {6: (), 7: (6, 7)}.get(q, (q,)):
+            dmas("w%d" % x, [("Y", T.G[127:128, PAD + 1024 * x:PAD + 1024 * x + 1024], T.LW[x], ["LW", "LWo", "g%d" % x, "g%d" % q],
+                              ["G%d" % x])])
     slot = {q: (h, sb + n) for ranks, h, sb, c0 in BATCH for n, q in enumerate(ranks)}
-    dmas("ldD", [("Y", T.Di[32 * slot[q][1] + 16 * kh:32 * slot[q][1] + 16 * kh + 8, 32 + 1024 * slot[q][0]:1056 + 1024 * slot[q][0]],
+    dmas("ldD", [("Y", T.Di[32 * slot[q][1] + 16 * kh:32 * slot[q][1] + 16 * kh + 8, 32 + DW * slot[q][0]:DW + DW * slot[q][0]],
                   inc_of(q)[0][q], [inc_of(q)[1], "Dz0", "Dz1"], ["D%d%d" % (kh, q)]) for q in range(8) for kh in range(2)])
     load_inc(1)
     dmas("ldW", [("Y", T.Wl[0:32, :], T.LW[:], ["LW", "LWo"], ["Wl"])])
     Gk = ["G%d" % q for q in range(8)]
-    Zk = ["Z%d" % j for j in range(16)]
-    Dk = ["D00", "Dpad"]
+    Zk = ["Z%d" % j for j in range(32)]
+    Dk = ["D00", "Dpad0", "Dpad1"]
     place = {q: (b, n) for b, (ranks, h, sb, c0) in enumerate(BATCH) for n, q in enumerate(ranks)}
 
     def key_cols(q, jj):
         b, n = place[q]
-        c = 16 * (len(BATCH[b][0]) * jj + n)
+        c = KW * (4 * n + jj)
         return bank(b, c, c + 16)
 
     def own_keys(t):
         for b, (ranks, h, sb, c0) in enumerate(BATCH):
-            w = 64 * len(ranks)
-            mm(bank(b, 0, w), T.onesb[0:16, :], T.pK[0:16, 0:w], ["onesb", "pK"], b, True, False)
+            w = 4 * KW * len(ranks)
+            mm(bank(b, 0, w), T.onesk[0:16, :], T.pK[0:16, 0:w], ["onesk", "pK"], b, True, False)
             for q in ranks:
                 for jj in range(4):
                     u = 1024 * q + 256 * jj
@@ -359,34 +383,29 @@ def rank_program(g, core, T, topo):
         ranks, h, sb, c0 = BATCH[b]
         n = len(ranks)
         B = str(b)
-        c, ct = slice(c0, c0 + 4 * n), slice(32 * t + c0, 32 * t + c0 + 4 * n)
-        mins = T.mins[:, 16 * c0:16 * c0 + 64 * n]
-        least = T.mins[:, 16 * c0 + 15:16 * c0 + 64 * n:16]
+        lo, hi = KW * c0, KW * (c0 + 4 * n)
+        least, whole, less = [T.mins[:, lo + x:hi:KW] for x in (15, 17, 18)]
+        reset = T.reset[:, 16 * KW * t:16 * KW * t + hi - lo]
         op("V", ["reset"], ["#" + B, "mins" + B],
-           lambda: V.tensor_tensor_scan(mins, T.reset[:, 0:64 * n], bank(b, 0, 64 * n), 0.0, A.add, A.min))
+           lambda: V.tensor_tensor_scan(T.mins[:, lo:hi], reset, bank(b, 0, hi - lo), 0.0, A.add, A.min))
         yield
-        cp(T.xi[:, c], least, ["mins" + B], ["xi" + B])
-        yield
-        z = 32 * b + 3 * n
-        tt(T.cand[:, z:z + 4 * n], T.xi[:, c], least, A.is_gt, ["xi" + B, "mins" + B], ["cand" + B])
+        qs = slice(ranks[0], ranks[0] + n)
+        tt(T.cand[:, qs, 4:8], whole, least, A.is_gt, ["mins" + B, "cand"], ["cand" + B])
         for s in range(4):
-            mm(bank(b, 256, 256 + 4 * n), T.TB[:] if s == 0 else T.onesb[:], T.cand[:, z - n * s:z + 4 * n - n * s],
+            mm(bank(b, POS, POS + 4 * n), T.TB[:] if s == 0 else T.onesb[:], T.cand[:, qs, 4 - s:8 - s],
                ["cand" + B, "TB", "onesb"], b, s == 0, s == 3)
         yield
-        tt(T.rr[:, ct], least, T.xi[:, c], A.subtract, ["xi" + B, "mins" + B], ["rr%d%d" % (t, b)])
-        yield
-        tt(T.zz[:, c], T.rr[:, ct], T.posc[:, ct], A.add, ["rr%d%d" % (t, b), "posc"], ["zz" + B])
+        z0, zk = 32 * t + c0, "zz%d%d" % (t, b)
+        tt(T.zz[:, z0:z0 + 4 * n], least, less, A.subtract, ["mins" + B], [zk])
         yield
         m = 32 * (sb + n)
         for jj in range(4):
-            p0 = 512 * b + 128 * jj
             for x in range(n):
-                j = n * jj + x
-                p = p0 + 32 * (sb + x)
-                ts(T.P[:, p:p + 32], T.iK[:], bank(b, 256 + j, 257 + j), A.is_equal, ["iK", "zz" + B],
-                   ["#" + B, "P%d_%d" % (b, j)], T.zz[:, c0 + j:c0 + j + 1], A.mult)
-            mm(T.ps[0:m, 512 * (3 + b):512 * (3 + b) + 8], T.P[:, p0:p0 + m], T.onesf[:],
-               ["P%d_%d" % (b, n * jj + x) for x in range(n)] + ["onesf", "Pz%d%d" % (b, jj)], 3 + b, jj == 0, jj == 3)
+                j = 4 * x + jj
+                ts(T.P[:, 4 * b + jj, 32 * (sb + x):32 * (sb + x) + 32], T.iK[:], bank(b, POS + j, POS + j + 1), A.is_equal,
+                   ["iK", zk], ["#" + B, "P%d_%d" % (b, j)], T.zz[:, z0 + j:z0 + j + 1], A.mult)
+            mm(T.ps[0:m, 512 * (3 + b):512 * (3 + b) + 8], T.P[:, 4 * b + jj, 0:m], T.onesf[:],
+               ["P%d_%d" % (b, 4 * x + jj) for x in range(n)] + ["onesf", "Pz%d" % b], 3 + b, jj == 0, jj == 3)
             yield
 
     def back(t, b):
@@ -395,7 +414,8 @@ def rank_program(g, core, T, topo):
         lo, m = 32 * sb, 32 * (sb + len(ranks))
         w = slice(128 * b + lo, 128 * b + m)
         bz, bo, bv = 3 + b, 6, 7
-        ts(T.L[0:m, 8 * b:8 * b + 8], T.ps[0:m, 512 * bz:512 * bz + 8], kF[0:m, 5:6], A.max, ["kF"], ["#%d" % bz, "L" + B])
+        ts(T.L[0:m, 8 * b:8 * b + 8], T.ps[0:m, 512 * bz:512 * bz + 8], 0.484375, A.add, ["kF"], ["#%d" % bz, "L" + B],
+           kF[0:m, 5:6], A.max)
         yield
         fr = T.fr[0:m, 2 * b:2 * b + 1]
         ts(fr, T.L[0:m, 8 * b:8 * b + 1], T.ps[0:m, 512 * bz:512 * bz + 1], A.subtract, ["L" + B], ["#%d" % bz, "fr" + B],
@@ -404,7 +424,7 @@ def rank_program(g, core, T, topo):
         mm(bank(bv, lo, m), T.onesm[0:m, :], T.E[0:m, w], ["onesm", "E" + B], bv)
         yield
         XL = T.XL[:, 128 * b:128 * b + 128]
-        tt(XL, T.Di[:, 0:DW].indirect(T.L[:, 8 * b:8 * b + 8]), T.maskR[:], A.mult, Dk + ["L" + B, "maskR"], ["XL" + B])
+        tt(XL, T.Di[:, DW * h:DW * h + DW].indirect(T.L[:, 8 * b:8 * b + 8]), T.maskR[:], A.mult, Dk + ["L" + B, "maskR"], ["XL" + B])
         k = (m - lo) // 16
         mm(bank(bo, 0, k), XL, T.Q8[:, lo // 16:m // 16], ["XL" + B, "Q8"], bo)
         act(T.vals[:, w], bank(bv, lo, m), F.Relu, ["bias2"], ["#%d" % bv, "vals" + B], bias=bias2)
@@ -418,23 +438,20 @@ def rank_program(g, core, T, topo):
 
     def movers(t, b):
         ranks, h, sb, c0 = BATCH[b]
-        act(T.le[:, 32 * t + c0:32 * t + c0 + 4 * len(ranks)], bank(b, 256, 256 + 4 * len(ranks)), F.Sign, ["lim"],
+        act(T.le[:, 32 * t + c0:32 * t + c0 + 4 * len(ranks)], bank(b, POS, POS + 4 * len(ranks)), F.Sign, ["lim"],
             ["#%d" % b, "le%d%d" % (t, b)], scale=-1.0, bias=lim)
 
+    tb = [(t, b) for t in range(2) for b in range(NB)]
+
     def new_parts():
-        tb = [(t, b) for t in range(2) for b in range(NB)]
-        tt(T.dd[:], T.rr[:], T.own32[:], A.subtract, ["rr%d%d" % x for x in tb] + ["own32"], ["dd"])
         tt(T.ee[:], T.le[:], T.dd[:], A.mult, ["le%d%d" % x for x in tb] + ["dd"], ["ee"])
         for t in range(2):
-            pn = T.ps[0:32, 512 * (4 + t):512 * (4 + t) + 128]
-            mm(pn, T.own[:, 32 * t:32 * t + 32], T.Idb[:], ["own", "Idb"], 4 + t, True, False)
-            mm(pn, T.dd[:, 32 * t:32 * t + 32], T.Id16[:], ["dd", "Id16"], 4 + t, False, False)
-            mm(pn, T.ee[:, 32 * t:32 * t + 32], T.Id16[:], ["ee", "Id16"], 4 + t, False, True)
-            act(T.ob[0:32, t:256:2], pn, F.Copy, [], ["#%d" % (4 + t), "ob%d" % t])
-        rows = [(ranks[0], len(ranks), jj, c0 + len(ranks) * jj) for ranks, h, sb, c0 in BATCH for jj in range(4)]
-        dmas("stN", [("Y", T.SN[q:q + n, 32 * jj:32 * jj + 32, :], T.ob[c:c + n, :], ["ob0", "ob1"], ["SN%d" % c])
-                     for q, n, jj, c in rows])
-        exchange(lambda q: T.SN[q], T.LN[me], "arrN", ["SN0"], "LN")
+            pn = T.ps[0:32, 512 * t:512 * t + 128]
+            mm(pn, T.own[:, 32 * t:32 * t + 32], T.Idb[:], ["own", "Idb"], t, True, False)
+            mm(pn, T.dd[:, 32 * t:32 * t + 32], T.Idb[:], ["dd", "Idb"], t, False, False)
+            mm(pn, T.ee[:, 32 * t:32 * t + 32], T.Idb[:], ["ee", "Idb"], t, False, True)
+            act(T.ob[0:32, t:256:2], pn, F.Identity, [], ["#%d" % t, "ob%d" % t], scale=16.0)
+        dmas("stN", [("Y", T.SN[:], T.ob[0:32, :], ["ob0", "ob1"], ["SN0"])])
 
     def fillers(t):
         for b in range(NB):
@@ -442,22 +459,28 @@ def rank_program(g, core, T, topo):
             yield
         if t == 0:
             lists(1)
-            act(T.junk[0:32, 0:256], T.Wl[0:32, :], F.Identity, ["Wl"], ["junk", "acc4"], scale=-15.0, accum_out=T.acc[0:32, 4:5])
+        else:
+            tt(T.dd[:], T.zz[:], T.ownp[:], A.subtract, ["zz%d%d" % x for x in tb] + ["ownp"], ["dd"])
+        yield
+        if t == 0:
+            act(T.junk[0:32, 0:256], T.Wl[0:32, :], F.Identity, ["Wl"], ["junk0", "acc7"], scale=-15.0, accum_out=T.acc[0:32, 7:8])
         else:
             new_parts()
         yield
 
     for t in range(2):
-        for j in range(16):
+        w = 256 if t else 512
+        for j in range(NV // w):
             b = j % 8
-            mm(bank(b), T.LZ[:], T.G[:, PAD + 512 * j:PAD + 512 * j + 512], LZk + ["G%d" % (j // 2)], b)
-            out = T.Z[:, 512 * j:512 * j + 512]
+            mm(bank(b, 0, w), T.LZ[:], T.G[:, PAD + w * j:PAD + w * j + w], LZk + ["G%d" % (w * j // 1024)], b)
+            out = T.Z[:, w * j:w * j + w]
+            keys = ["#%d" % b] + Zk[w * j // 256:w * (j + 1) // 256]
             if t == 0 and j == 9:
                 lists(0)
             if j % 2:
-                ts(out, bank(b), 0.0, A.max, [], ["#%d" % b, "Z%d" % j])
+                ts(out, bank(b, 0, w), 0.0, A.max, [], keys)
             else:
-                act(out, bank(b), F.Relu, [], ["#%d" % b, "Z%d" % j])
+                act(out, bank(b, 0, w), F.Relu, [], keys)
         own_keys(t)
         left = [4 * len(b[0]) for b in BATCH]
         steps = {"v": gathers(t, "V", PIECES["V"], left), "s": gathers(t, "S", PIECES["S"], left), "x": fillers(t)}
@@ -470,15 +493,17 @@ def rank_program(g, core, T, topo):
 
     e0 = PAD
     for r, n in enumerate(CUT):
+        b = 2 + r
         for x in range(n):
-            mm(bank(r, 16 * x, 16 * x + 16), T.G[:, e0:e0 + 128], T.LC[:], Gk + ["LC"], r)
+            mm(bank(b, 16 * x, 16 * x + 16), T.G[:, e0:e0 + 128], T.LC[:], Gk + ["LC"], b)
             e0 += 128
-        act(T.junk[:, 0:16 * n], bank(r, 0, 16 * n), F.Relu, [], ["#%d" % r, "junk", "acc%d" % r], accum_out=T.acc[:, r:r + 1])
-    pcut = T.ps[0:1, 512 * 6:512 * 6 + 8]
-    mm(pcut, T.onesf[:, 0:1], T.acc[:], ["onesf", "acc0", "acc1", "acc2", "acc3", "acc4"], 6)
-    op("V", [], ["#6", "cb"], lambda: V.tensor_reduce(T.cb[0:1, 0:1], pcut, AxisListType.X, A.add, negate=True))
-    dmas("stU", [("S", T.SU[:], T.cb[0:1, :], ["cb"], ["SU"])])
-    exchange(lambda q: T.SU[:], T.LU[me], "arrU", ["SU"], "LU")
+        act(T.junk[:, 256 * r:256 * r + 16 * n], bank(b, 0, 16 * n), F.Relu, [], ["#%d" % b, "junk%d" % r, "acc%d" % r],
+            accum_out=T.acc[:, r:r + 1])
+    pcut = T.ps[0:1, 0:8]
+    mm(pcut, T.onesf[:, 0:1], T.acc[:], ["onesf"] + acck, 0)
+    op("V", [], ["#0", "cb"], lambda: V.tensor_reduce(T.cb[0:1, 0:1], pcut, AxisListType.X, A.add, negate=True))
+    exchange(lambda q: T.SN[q], T.LN[me], "arrN", ["SN0"], "LN")
+    send([(far, T.cb[:, 0:1], far_eng), (near, T.cb[:, 0:1], [near_eng[0], near_eng[-1]])], T.CU[:, me:me + 1], "arrU", ["cb"], "LU")
 
     outs = [("Y", T.newpart[me:me + 1, :], T.SN[me], ["SN0"], ["o0"])]
     if me > 0:
@@ -487,6 +512,6 @@ def rank_program(g, core, T, topo):
         outs.append(("Y", T.newpart[me + 1:N, :], T.LN[me + 1:N], ["LN"], ["o2"]))
     dmas("outN", outs)
     dmas("outU", [("S", T.cut[me:me + 1, :], T.cb[0:1, 0:1], ["cb"], ["u"])]
-         + [("Y" if n % 2 == 0 else "S", T.cut[q:q + 1, :], T.LU[q, 0:1, 0:1], ["LU"], ["u%d" % q]) for n, q in enumerate(peers)])
+         + [(e, T.cut[lo:hi, :], T.CU[0:1, lo:hi], ["LU"], ["u" + e]) for e, lo, hi in (("Y", 0, me), ("S", me + 1, N)) if lo < hi])
     for s in total:
         g.wait_ge(T.sem[s], total[s])

from concourse.bass import DstId, RemoteDMATransfer
from concourse.mybir import AluOpType, AxisListType, ActivationFunctionType

PAD = 288
NV = 8192
KW = 19
POS = 320
DW = 32 + 1024
BATCH = (((0, 1, 2, 3), 0, 0, 0), ((4, 5), 1, 2, 16), ((6, 7), 1, 0, 24))
ORDER = "vsvsvsvAAAssAABABBAssBBBsaxBaaCbCxCbabCCCCacbccxxbcxc"
PIECES = {"V": ((0, (0, 1)), (2, (0,)), (2, (1,)), (4, (0,))),
          "S": ((1, (0, 1)), (3, (0,)), (3, (1,)), (4, (1,)), (5, (0, 1)), (6, (0, 1)), (7, (0,)), (7, (1,)))}
SHIFT = 192
SEL = 22
CUT = (16, 16, 12, 10, 6, 4)

SCRATCH = {
    "SA": ("dram", [4, 128, 16], "int32"), "LA": ("dram", [8, 128, 16], "int32"),
    "SW": ("dram", [8, 128, 8], "bfloat16"), "LW": ("dram", [8, 128, 8], "bfloat16"),
    "SP": ("dram", [8, 128, 64], "uint16"), "LP": ("dram", [8, 128, 64], "uint16"),
    "SI": ("dram", [8, 128, 64], "int32"), "LI": ("dram", [8, 128, 64], "int32"),
    "SN": ("dram", [8, 128, 8], "float32"), "LN": ("dram", [8, 128, 8], "float32"),
    "win": ("sbuf", [128, NV], "bfloat16"), "G": ("sbuf", [128, PAD + NV], "bfloat16"),
    "Z": ("sbuf", [128, NV], "bfloat16"), "Y": ("sbuf", [128, 4096], "bfloat16"),
    "Di": ("sbuf", [128, 2 * DW], "int32"), "P": ("sbuf", [128, 12, 128], "float32"),
    "pinI": ("sbuf", [128, 512], "int32"), "incI": ("sbuf", [128, 512], "int32"),
    "pinS": ("sbuf", [128, 512], "uint16"), "pinU": ("sbuf", [128, 512], "uint16"), "incU": ("sbuf", [128, 512], "uint16"),
    "Ai": ("sbuf", [128, 256], "int32"), "Wi": ("sbuf", [128, 256], "int32"), "Ao": ("sbuf", [128, 256], "int32"),
    "Ab": ("sbuf", [128, 256], "bfloat16"), "Wb": ("sbuf", [128, 256], "bfloat16"), "Aob": ("sbuf", [128, 256], "bfloat16"),
    "Wl": ("sbuf", [128, 256], "bfloat16"), "junk": ("sbuf", [128, 1536], "bfloat16"),
    "Sel": ("sbuf", [128, 4096], "bfloat16"), "reset": ("sbuf", [128, 32 * KW], "float32"),
    "pK": ("sbuf", [128, 16 * KW], "bfloat16"), "onesk": ("sbuf", [128, 128], "bfloat16"),
    "kI": ("sbuf", [128, 8], "int32"), "kF": ("sbuf", [128, 32], "float32"), "iM": ("sbuf", [128, 128], "float32"),
    "i32": ("sbuf", [128, 32], "float32"), "iK": ("sbuf", [128, 32], "float32"), "posc": ("sbuf", [128, 2, 32], "float32"),
    "posb": ("sbuf", [128, 64], "float32"),
    "Idb": ("sbuf", [128, 128], "bfloat16"), "Id32": ("sbuf", [128, 32], "float32"), "TB": ("sbuf", [128, 128], "bfloat16"),
    "t0": ("sbuf", [128, 128], "bfloat16"), "Ib": ("sbuf", [128, 32], "bfloat16"),
    "onesb": ("sbuf", [128, 128], "bfloat16"), "onesm": ("sbuf", [128, 128], "bfloat16"), "onesf": ("sbuf", [128, 8], "float32"),
    "maskR": ("sbuf", [128, 128], "float32"), "Q8": ("sbuf", [128, 8], "float32"), "NE": ("sbuf", [128, 8], "float32"),
    "SelS": ("sbuf", [128, 16], "bfloat16"), "LZ": ("sbuf", [128, 128], "bfloat16"),
    "LC": ("sbuf", [128, 16], "bfloat16"), "LO": ("sbuf", [128, 16], "bfloat16"), "f": ("sbuf", [128, 256], "float32"),
    "own": ("sbuf", [128, 64], "bfloat16"), "own32": ("sbuf", [128, 64], "float32"), "mins": ("sbuf", [128, 32 * KW], "float32"),
    "cand": ("sbuf", [128, 8, 8], "bfloat16"), "ownp": ("sbuf", [128, 64], "float32"),
    "zz": ("sbuf", [128, 64], "float32"), "dd": ("sbuf", [128, 64], "bfloat16"), "le": ("sbuf", [128, 64], "float32"),
    "ee": ("sbuf", [128, 64], "bfloat16"),
    "L": ("sbuf", [128, 24], "uint16"), "XL": ("sbuf", [128, 384], "float32"), "fr": ("sbuf", [128, 8], "float32"),
    "E": ("sbuf", [128, 384], "bfloat16"), "off": ("sbuf", [128, 24], "uint16"),
    "vals": ("sbuf", [128, 384], "bfloat16"), "old": ("sbuf", [128, 384], "bfloat16"),
    "ob": ("sbuf", [128, 256], "float32"), "acc": ("sbuf", [128, 8], "float32"), "cb": ("sbuf", [128, 8], "float32"),
    "CU": ("sbuf", [128, 8], "float32"),
    "ps": ("psum", [128, 4096], "float32"),
}
SEMAPHORES = (["cV", "cS", "cT", "cG", "stA", "stP", "stI", "stW", "ownA", "arrA", "arrP", "arrW", "arrI", "arrN", "arrU", "sent",
               "ldO", "ldN", "ldV", "ldA", "ldW", "ldP", "ldI0", "ldI1", "ldD", "stN", "outN", "outU"]
              + ["w%d" % q for q in range(8)])

A = AluOpType
F = ActivationFunctionType


def rank_program(g, core, T, topo):
    me = T.rank_of(core)
    if me is None:
        return
    cores = list(T.cores)
    N = len(cores)
    NB = len(BATCH)
    Q = {"V": g.vector, "S": g.scalar, "T": g.tensor, "G": g, "Y": g.sync}
    total = {}
    seen = {e: {} for e in Q}
    wrote, read = {}, {}

    def wait(e, tok):
        if seen[e].get(tok[1], 0) < tok[2]:
            Q[e].wait_ge(T.sem[tok[1]], tok[2])
            seen[e][tok[1]] = tok[2]

    def order(e, rd, wr):
        for k in rd:
            if k in wrote:
                wait(e, wrote[k])
        for k in wr:
            if k in wrote and not (wrote[k][0] == e and (e == "T" or k[0] == "#")):
                wait(e, wrote[k])
            for tok in read.get(k, []):
                if tok[0] != e:
                    wait(e, tok)

    def done(tok, rd, wr):
        for k in rd:
            read.setdefault(k, []).append(tok)
        for k in wr:
            wrote[k] = tok
            read[k] = []

    def op(e, rd, wr, call):
        order(e, rd, wr)
        s = "c" + e
        total[s] = total.get(s, 0) + 1
        call().then_inc(T.sem[s], 1)
        done((e, s, total[s]), rd, wr)

    def dmas(sem, items):
        end = total.get(sem, 0) + 16 * len(items)
        for e, out, src, rd, wr in items:
            order(e, rd, wr)
            Q[e].dma_start(out, src).then_inc(T.sem[sem], 16)
        total[sem] = end
        for e, out, src, rd, wr in items:
            done(("dma", sem, end), rd, wr)

    peers = [(me + d) % N for d in range(1, N)]
    near = [q for q in peers if topo.chip(cores[q]) == topo.chip(core)]
    far = [q for q in peers if q not in near]
    far_eng = topo.engines(core, cores[far[0]])
    near_eng = [x for x in topo.engines(core, cores[near[0]]) if x not in far_eng]
    chips = sorted(set(topo.chip(c) for c in cores))
    on_chip = [[q for q in range(N) if topo.chip(cores[q]) == c] for c in chips]

    def send(transfers, dst, arr, rd, landed):
        order("G", rd, [])
        trs = []
        for ranks, src, engines in transfers:
            ids = [DstId(rid=topo.addr(cores[q])[0], pnc=topo.addr(cores[q])[1]) for q in ranks]
            trs.append(RemoteDMATransfer(dst_ids=ids, dma_engine_mask=sum(1 << x for x in engines), remote_sem=T.sem[arr],
                                         srcs=[src], dsts=[dst] * len(ranks)))
        g.remote_dma_fused(trs, local_sem=T.sem.sent)
        total["sent"] = total.get("sent", 0) + sum(len(x[2]) for x in transfers)
        total[arr] = sum(len(x[0]) * len(x[2]) for x in transfers)
        wrote[landed] = ("far", arr, total[arr])

    def exchange(src_of, dst, arr, rd, landed, last=False):
        fe, ne = (far_eng[-len(far):], near_eng[-len(near):]) if last else (far_eng, near_eng)
        send([([q], src_of(q), [x]) for q, x in list(zip(far, fe)) + list(zip(near, ne))], dst, arr, rd, landed)

    V, S, PE = g.vector, g.scalar, g.tensor

    def ts(out, in0, s1, op0, rd, wr, s2=None, op1=None):
        if op1 is None:
            op("V", rd, wr, lambda: V.tensor_scalar(out, in0, s1, None, op0))
        else:
            op("V", rd, wr, lambda: V.tensor_scalar(out, in0, s1, s2, op0, op1))

    def tt(out, in0, in1, o, rd, wr):
        op("V", rd, wr, lambda: V.tensor_tensor(out, in0, in1, o))

    def cp(out, in_, rd, wr):
        op("V", rd, wr, lambda: V.tensor_copy(out, in_))

    def fill(ap, c, wr):
        op("V", [], wr, lambda: V.memset(ap, c))

    def act(out, in_, fn, rd, wr, **kw):
        op("S", rd, wr, lambda: S.activation(out, in_, fn, **kw))

    def mm(out, lhsT, rhs, rd, bank, start=True, stop=True):
        op("T", rd, ["#%d" % bank], lambda: PE.matmul(out, lhsT, rhs, start, stop))

    def iota(out, pattern, base, cm, key, flt=True):
        if flt:
            op("G", [], [key], lambda: g.iota(out, pattern, base, cm, allow_small_or_imprecise_dtypes=True))
        else:
            op("G", [], [key], lambda: g.iota(out, pattern, base, cm))

    def select(out, in_, cmp, x, rd, key):
        op("G", rd, [key], lambda: g.affine_select(out, in_, [[1, 128]], cmp, x, 0, -1))

    def bank(b, lo=0, hi=512):
        return T.ps[:, 512 * b + lo:512 * b + hi]

    dmas("stA", [("Y", T.SA[:], T.part[:], [], ["SA"])])
    dmas("ldO", [("S", T.Ao[0:4, :], T.part[me:me + 1, :], [], ["Ao"])])
    dmas("ldN", [("Y", T.pinI[:], T.pin[:], [], ["pinI"])])
    dmas("ldV", [("S", T.Wi[0:32, :], T.w[:], [], ["Wi"])])
    mine = chips.index(topo.chip(core))
    rows = slice(64 * on_chip[mine].index(me), 64 * on_chip[mine].index(me) + 64)
    dmas("ownA", [("S", T.LA[me, rows, :], T.part[me:me + 1, :], [], ["LAo"])])

    iota(T.kI[:, 0:1], [[0, 1]], 0, 1, "k", flt=False)
    iota(T.i32[:], [[1, 32]], 0, 0, "i32")
    others = [k for k in range(len(chips)) if me not in on_chip[k]]
    send([(on_chip[k], T.SA[k], [far_eng[2 * n]]) for n, k in enumerate(others)] + [(near, T.SA[mine], near_eng[:1])],
         T.LA[me], "arrA", ["SA"], "LA")

    kF = T.kF
    i16 = T.i32[:, 0:16]

    def col(j):
        return kF[:, j:j + 1]

    def blk(j):
        return T.f[:, 16 * j:16 * j + 16]

    c15, c127, z0, cm, pc, b0, spec, bias, bias2, lim = [col(j) for j in range(8, 18)]
    fill(T.onesb[:], 1.0, ["onesb"])
    fill(T.onesm[:], 1.0, ["onesm"])
    fill(T.onesk[0:16, :], 2.0 ** -10, ["onesk"])
    fill(T.onesm[:, 15:128:16], 0.0, ["onesm"])
    ts(T.kI[:, 1:2], T.kI[:, 0:1], 15, A.bitwise_and, ["k"], ["k1"])
    ts(T.kI[:, 2:3], T.kI[:, 0:1], 4, A.arith_shift_right, ["k"], ["k2"])
    ts(T.kI[:, 3:4], T.kI[:, 0:1], 7, A.bitwise_and, ["k"], ["k3"])
    ts(T.kI[:, 4:5], T.kI[:, 0:1], 3, A.arith_shift_right, ["k"], ["k4"])
    ts(T.kI[:, 5:6], T.kI[:, 0:1], 31, A.bitwise_and, ["k"], ["k5"])
    fill(T.L[:], 0, ["L0", "L1", "L2"])
    cp(kF[:, 0:6], T.kI[:, 0:6], ["k", "k1", "k2", "k3", "k4", "k5"], ["kF"])
    fill(lim, -992.5, ["lim"])
    ts(T.Id32[:], T.i32[:], col(0), A.is_equal, ["i32", "kF"], ["Id32"])
    ts(c15, col(0), 15.0, A.is_equal, ["kF"], ["c15"])
    ts(cm, col(1), 15.0, A.not_equal, ["kF"], ["cm"], -16.0, A.mult)
    ts(c127, col(0), 127.0, A.is_equal, ["kF"], ["c127"])
    ts(z0, col(1), 0.0, A.is_equal, ["kF"], ["z0"])
    ts(b0, col(1), cm, A.mult, ["kF", "cm"], ["b0"], 0.0625, A.mult)
    ts(pc, col(3), 128.0, A.mult, ["kF"], ["pc"], col(4), A.add)
    ts(blk(0), i16, col(1), A.subtract, ["i32", "kF"], ["d"])
    tt(bias, b0, c15, A.add, ["b0", "c15"], ["bias"])
    ts(T.Q8[:], T.i32[:, 0:8], col(2), A.is_equal, ["i32", "kF"], ["Q8"])
    ts(T.SelS[:], i16, col(1), A.is_equal, ["i32", "kF"], ["SelS"])
    tt(spec, c15, c127, A.add, ["c15", "c127"], ["spec"])
    tt(blk(1), blk(0), blk(0), A.mult, ["d"], ["d2"])
    ts(blk(2), blk(0), 0.0, A.is_equal, ["d"], ["a0"], -2.0, A.mult)
    ts(blk(3), i16, 0.0, A.is_equal, ["i32", "c15"], ["p0"], c15, A.mult)
    cp(T.Aob[0:4, :], T.Ao[0:4, :], ["Ao"], ["Aob"])
    cp(T.pinS[:], T.pinI[:], ["pinI"], ["pinS"])
    dmas("stP", [("Y", T.SP[:, 16 * i:16 * i + 16, :], T.pinS[:, 64 * i:64 * i + 64], ["pinS"], ["SP%d" % i]) for i in range(8)])
    iota(T.posb[:], [[64, 2], [0, 8], [16, 4]], 32, 0, "posb")
    iota(T.iM[:], [[1, 8], [0, 16]], 0, 0, "iM")
    select(T.Idb[:], T.onesb[:], A.is_equal, 0.0, ["onesb"], "Idb")
    exchange(lambda q: T.SP[q], T.LP[me], "arrP", ["SP0"], "LP")
    cp(T.Wb[0:32, :], T.Wi[0:32, :], ["Wi"], ["Wb"])
    dmas("stW", [("Y", T.SW[:], T.Wb[0:32, :], ["Wb"], ["SW"]), ("Y", T.LW[me], T.Wb[4 * me:4 * me + 4, :], ["Wb"], ["LWo"])])

    for h in range(2):
        iota(T.Di[:, DW * h:DW * h + 32], [[1, 32]], -PAD, 2, "Dpad%d" % h, flt=False)
        iota(T.Di[:, DW * h + 32:DW * h + DW], [[0, 1024]], 0, 0, "Dz%d" % h, flt=False)
        if h == 0:
            exchange(lambda q: T.SW[q], T.LW[me], "arrW", ["SW"], "LW", last=True)
    select(T.t0[:], T.onesb[:], A.is_gt, 0.0, ["onesb"], "t0")
    iota(T.iK[:], [[1, 32]], -1024, 0, "iK")
    select(T.TB[:], T.t0[:], A.not_equal, -1024.0, ["t0"], "TB")

    for j in range(SEL):
        act(T.Sel[0:32, 128 * j:128 * j + 128], T.onesm[0:32, :], F.Identity, ["onesm", "Id32"], ["Sel%d" % j],
            scale=T.Id32[0:32, j:j + 1])

    def window(j, b, e, rows, r, src, key):
        mm(bank(b, 0, 256), T.Sel[0:rows, 128 * r:128 * r + 128], src[0:rows, :], ["Sel%d" % r, key], b)
        out = T.win[:, 256 * j:256 * j + 256]
        if e == "V":
            ts(out, bank(b, 0, 256), bias, A.add, ["bias"], ["#%d" % b, "win%d" % j], 0.0, A.max)
        else:
            act(out, bank(b, 0, 256), F.Relu, ["bias"], ["#%d" % b, "win%d" % j], bias=bias)

    ts(bias2, cm, -0.96875, A.mult, ["cm", "bias"], ["bias2"], bias, A.add)
    ts(blk(5), blk(1), 1.0, A.is_equal, ["d2"], ["a1"])
    ts(T.NE[:], T.i32[:, 0:8], col(2), A.not_equal, ["i32", "kF", "spec"], ["NE"], spec, A.max)
    ts(blk(6), blk(3), -128.0, A.mult, ["p0"], ["pC"], c127, A.add)
    ts(blk(7), blk(3), -112.0, A.mult, ["p0"], ["pZ"], c127, A.add)
    ts(blk(8), blk(3), -0.5, A.mult, ["p0"], ["pO"])
    tt(blk(9), blk(5), blk(2), A.add, ["a1", "a0"], ["F"])
    cp(T.Ib[0:32, :], T.Id32[0:32, :], ["Id32"], ["Ib"])
    ts(T.f[:, 144:145], T.f[:, 144:145], z0, A.add, ["F", "z0"], ["F"])
    for j in range(SEL, 32):
        ts(T.Sel[0:32, 128 * j:128 * j + 128], T.onesm[0:32, :], T.Ib[0:32, j:j + 1], A.mult, ["onesm", "Ib"], ["Sel%d" % j])
    ts(blk(11), blk(9), cm, A.mult, ["F", "cm"], ["Fm"])
    for r in range(2):
        window(4 * me + r, r, "V", 4, r, T.Aob, "Aob")
    tt(T.LC[:], blk(11), blk(6), A.add, ["Fm", "pC"], ["LC"])
    ts(blk(10), blk(11), 0.03125, A.mult, ["Fm"], ["Fo"])
    tt(blk(12), blk(11), blk(7), A.add, ["Fm", "pZ"], ["FZ"])
    tt(T.LO[:], blk(10), blk(8), A.add, ["Fo", "pO"], ["LO"])
    for r in range(2, 4):
        window(4 * me + r, r, "S", 4, r, T.Aob, "Aob")
    for i in range(8):
        act(T.LZ[:, 16 * i:16 * i + 16], blk(12), F.Identity, ["FZ", "NE"], ["LZ%d" % i], scale=T.NE[:, i:i + 1])
    ts(T.posc[:], T.posb[:], pc, A.add, ["posb", "pc"], ["posc"])
    ts(T.maskR[:], T.iM[:], col(1), A.is_equal, ["iM", "kF"], ["maskR"])
    LZk = ["LZ%d" % i for i in range(8)]

    first = [me] + peers
    dmas("ldA", [("Y", T.Ai[0:32, :], T.LA[:, rows, :], ["LA", "LAo"], ["Ai"])])
    dmas("ldP", [("Y", T.pinU[:, 64 * q:64 * q + 64], T.SP[q] if q == me else T.LP[q], ["SP0" if q == me else "LP"], ["pinU%d" % q])
                 for q in first])
    dmas("stI", [("Y", T.SI[:, 16 * i:16 * i + 16, :], T.inc[:, 64 * i:64 * i + 64], ["LP"], ["SI%d" % i]) for i in range(8)])
    exchange(lambda q: T.SI[q], T.LI[me], "arrI", ["SI0"], "LI")
    iota(T.reset[:], [[0, 32 * KW]], 0, 0, "reset")
    for c, x in ((0, 1 << 20), (16, -3 << 22), (17, 3 << 22)):
        iota(T.reset[:, c:32 * KW:KW], [[0, 32]], x, 0, "reset")
    iota(T.pK[0:16, :], [[0, 16], [2, KW]], 33, 0, "pK")
    for c in (17, 18):
        iota(T.pK[0:16, c:16 * KW:KW], [[0, 16]], 8192, 0, "pK")
    iota(T.cand[:], [[0, 64]], 0, 0, "cand")
    iota(T.onesf[:], [[0, 8]], 1, 0, "onesf")
    for b, (ranks, h, sb, c0) in enumerate(BATCH):
        if sb:
            iota(T.P[:, 4 * b:4 * b + 4, 0:32 * sb], [[0, 128 * sb]], 0, 0, "Pz%d" % b)
    iota(T.G[:, 0:PAD], [[0, PAD]], 0, 0, "Gpad")
    iota(T.acc[:], [[0, 8]], 0, 0, "acc7")
    iota(T.cb[:], [[0, 8]], 0, 0, "cb")
    acck = ["acc%d" % r for r in range(8)]
    for k in acck:
        wrote[k] = wrote["acc7"]

    def inc_of(q):
        return (T.SI, "SI0") if q == me else (T.LI, "LI")

    def load_inc(t):
        dmas("ldI%d" % t, [("Y", T.incI[:, 256 * t + 32 * q:256 * t + 32 * q + 32], inc_of(q)[0][q, t:128:2, :], [inc_of(q)[1]],
                            ["incI%d%d" % (t, q)]) for q in first])

    def lists(t):
        cp(T.incU[:, 256 * t:256 * t + 256], T.incI[:, 256 * t:256 * t + 256], ["incI%d0" % t], ["incU%d" % t])

    cp(T.Ab[0:32, :], T.Ai[0:32, :], ["Ai"], ["Ab"])
    for n, j in enumerate([j for j in range(32) if j // 4 != me]):
        window(j, (n + 4) % 8, "V" if n % 2 else "S", 32, j, T.Ab, "Ab")
    wink = ["win%d" % j for j in range(32)]
    for t in range(2):
        mm(bank(1, 32 * t, 32 * t + 32), T.Ab[0:32, t:256:2], T.Idb[0:32, 0:32], ["Ab", "Idb"], 1)

    ends = [1024 * q for q in range(7)] + [7168 - SHIFT, NV]
    for q in range(8):
        lo, hi = ends[q], ends[q + 1]
        out = T.G[:, PAD + lo:PAD + hi]
        src = T.win[:, 0:NV].indirect(T.pinU[:, lo // 16:hi // 16])
        if q % 2 == 0:
            cp(out, src, wink + ["pinU0", "LP"], ["g%d" % q])
        else:
            act(out, src, F.Copy, wink + ["pinU0", "LP"], ["g%d" % q])
        if q == 0:
            ts(T.own[:], bank(1, 0, 64), 0.0625, A.mult, [], ["#1", "own"])
            ts(T.own32[:], bank(1, 0, 64), -15.5, A.add, [], ["#1", "own32"], 0.03125, A.mult)
        if q == 2:
            tt(T.ownp[:], T.own32[:], T.posc[:], A.add, ["own32", "posc"], ["ownp"])
        if q == 6:
            ts(T.reset[:, 18:32 * KW:KW], T.posc[:, :, 0:16], -1.0, A.mult, ["posc"], ["reset"])
            load_inc(0)
        for x in {6: (), 7: (6, 7)}.get(q, (q,)):
            dmas("w%d" % x, [("Y", T.G[127:128, PAD + 1024 * x:PAD + 1024 * x + 1024], T.LW[x], ["LW", "LWo", "g%d" % x, "g%d" % q],
                              ["G%d" % x])])
    slot = {q: (h, sb + n) for ranks, h, sb, c0 in BATCH for n, q in enumerate(ranks)}
    dmas("ldD", [("Y", T.Di[32 * slot[q][1] + 16 * kh:32 * slot[q][1] + 16 * kh + 8, 32 + DW * slot[q][0]:DW + DW * slot[q][0]],
                  inc_of(q)[0][q], [inc_of(q)[1], "Dz0", "Dz1"], ["D%d%d" % (kh, q)]) for q in range(8) for kh in range(2)])
    load_inc(1)
    dmas("ldW", [("Y", T.Wl[0:32, :], T.LW[:], ["LW", "LWo"], ["Wl"])])
    Gk = ["G%d" % q for q in range(8)]
    Zk = ["Z%d" % j for j in range(32)]
    Dk = ["D00", "Dpad0", "Dpad1"]
    place = {q: (b, n) for b, (ranks, h, sb, c0) in enumerate(BATCH) for n, q in enumerate(ranks)}

    def key_cols(q, jj):
        b, n = place[q]
        c = KW * (4 * n + jj)
        return bank(b, c, c + 16)

    def own_keys(t):
        for b, (ranks, h, sb, c0) in enumerate(BATCH):
            w = 4 * KW * len(ranks)
            mm(bank(b, 0, w), T.onesk[0:16, :], T.pK[0:16, 0:w], ["onesk", "pK"], b, True, False)
            for q in ranks:
                for jj in range(4):
                    u = 1024 * q + 256 * jj
                    mm(key_cols(q, jj), T.win[0:16, u + t:u + 256:2], T.LO[0:16, :], wink + ["LO"], b, False, False)

    def gathers(t, e, pieces, left):
        for q, xs in pieces:
            lo, hi = 16 * xs[0], 16 * xs[-1] + 16
            out = T.Y[:, 512 * q + 16 * lo:512 * q + 16 * hi]
            src = T.Z[:, 0:NV].indirect(T.incU[:, 256 * t + 32 * q + lo:256 * t + 32 * q + hi])
            keys = ["Y%d%d" % (q, x) for x in xs]
            if e == "S":
                act(out, src, F.Copy, Zk + ["incU%d" % t], keys)
            else:
                cp(out, src, Zk + ["incU%d" % t], keys)
            b = place[q][0]
            for x in xs:
                n = 512 * q + 256 * x
                for y in range(2):
                    left[b] -= 1
                    mm(key_cols(q, x + 2 * y), T.Y[:, n + y:n + 256:2], T.SelS[:], ["Y%d%d" % (q, x), "SelS"], b, False, left[b] == 0)
            yield

    def front(t, b):
        ranks, h, sb, c0 = BATCH[b]
        n = len(ranks)
        B = str(b)
        lo, hi = KW * c0, KW * (c0 + 4 * n)
        least, whole, less = [T.mins[:, lo + x:hi:KW] for x in (15, 17, 18)]
        reset = T.reset[:, 16 * KW * t:16 * KW * t + hi - lo]
        op("V", ["reset"], ["#" + B, "mins" + B],
           lambda: V.tensor_tensor_scan(T.mins[:, lo:hi], reset, bank(b, 0, hi - lo), 0.0, A.add, A.min))
        yield
        qs = slice(ranks[0], ranks[0] + n)
        tt(T.cand[:, qs, 4:8], whole, least, A.is_gt, ["mins" + B, "cand"], ["cand" + B])
        for s in range(4):
            mm(bank(b, POS, POS + 4 * n), T.TB[:] if s == 0 else T.onesb[:], T.cand[:, qs, 4 - s:8 - s],
               ["cand" + B, "TB", "onesb"], b, s == 0, s == 3)
        yield
        z0, zk = 32 * t + c0, "zz%d%d" % (t, b)
        tt(T.zz[:, z0:z0 + 4 * n], least, less, A.subtract, ["mins" + B], [zk])
        yield
        m = 32 * (sb + n)
        for jj in range(4):
            for x in range(n):
                j = 4 * x + jj
                ts(T.P[:, 4 * b + jj, 32 * (sb + x):32 * (sb + x) + 32], T.iK[:], bank(b, POS + j, POS + j + 1), A.is_equal,
                   ["iK", zk], ["#" + B, "P%d_%d" % (b, j)], T.zz[:, z0 + j:z0 + j + 1], A.mult)
            mm(T.ps[0:m, 512 * (3 + b):512 * (3 + b) + 8], T.P[:, 4 * b + jj, 0:m], T.onesf[:],
               ["P%d_%d" % (b, 4 * x + jj) for x in range(n)] + ["onesf", "Pz%d" % b], 3 + b, jj == 0, jj == 3)
            yield

    def back(t, b):
        ranks, h, sb, c0 = BATCH[b]
        B = str(b)
        lo, m = 32 * sb, 32 * (sb + len(ranks))
        w = slice(128 * b + lo, 128 * b + m)
        bz, bo, bv = 3 + b, 6, 7
        ts(T.L[0:m, 8 * b:8 * b + 8], T.ps[0:m, 512 * bz:512 * bz + 8], 0.484375, A.add, ["kF"], ["#%d" % bz, "L" + B],
           kF[0:m, 5:6], A.max)
        yield
        fr = T.fr[0:m, 2 * b:2 * b + 1]
        ts(fr, T.L[0:m, 8 * b:8 * b + 1], T.ps[0:m, 512 * bz:512 * bz + 1], A.subtract, ["L" + B], ["#%d" % bz, "fr" + B],
           -32.0, A.mult)
        act(T.E[0:m, w], T.Idb[0:m, lo:m], F.Identity, ["Idb", "fr" + B], ["E" + B], scale=fr)
        mm(bank(bv, lo, m), T.onesm[0:m, :], T.E[0:m, w], ["onesm", "E" + B], bv)
        yield
        XL = T.XL[:, 128 * b:128 * b + 128]
        tt(XL, T.Di[:, DW * h:DW * h + DW].indirect(T.L[:, 8 * b:8 * b + 8]), T.maskR[:], A.mult, Dk + ["L" + B, "maskR"], ["XL" + B])
        k = (m - lo) // 16
        mm(bank(bo, 0, k), XL, T.Q8[:, lo // 16:m // 16], ["XL" + B, "Q8"], bo)
        act(T.vals[:, w], bank(bv, lo, m), F.Relu, ["bias2"], ["#%d" % bv, "vals" + B], bias=bias2)
        yield
        off = T.off[:, 8 * b:8 * b + k]
        ts(off, bank(bo, 0, k), float(PAD), A.add, [], ["#%d" % bo, "off" + B])
        act(T.old[:, w], T.G[:, 0:PAD + NV].indirect(off), F.Identity, Gk + ["Gpad", "off" + B, "c127"], ["old" + B], scale=c127)
        yield
        tt(T.G[:, 0:PAD + NV].indirect(off), T.old[:, w], T.vals[:, w], A.add, ["old" + B, "vals" + B, "off" + B], Gk + ["Gpad"])
        yield

    def movers(t, b):
        ranks, h, sb, c0 = BATCH[b]
        act(T.le[:, 32 * t + c0:32 * t + c0 + 4 * len(ranks)], bank(b, POS, POS + 4 * len(ranks)), F.Sign, ["lim"],
            ["#%d" % b, "le%d%d" % (t, b)], scale=-1.0, bias=lim)

    tb = [(t, b) for t in range(2) for b in range(NB)]

    def new_parts():
        tt(T.ee[:], T.le[:], T.dd[:], A.mult, ["le%d%d" % x for x in tb] + ["dd"], ["ee"])
        for t in range(2):
            pn = T.ps[0:32, 512 * t:512 * t + 128]
            mm(pn, T.own[:, 32 * t:32 * t + 32], T.Idb[:], ["own", "Idb"], t, True, False)
            mm(pn, T.dd[:, 32 * t:32 * t + 32], T.Idb[:], ["dd", "Idb"], t, False, False)
            mm(pn, T.ee[:, 32 * t:32 * t + 32], T.Idb[:], ["ee", "Idb"], t, False, True)
            act(T.ob[0:32, t:256:2], pn, F.Identity, [], ["#%d" % t, "ob%d" % t], scale=16.0)
        dmas("stN", [("Y", T.SN[:], T.ob[0:32, :], ["ob0", "ob1"], ["SN0"])])

    def fillers(t):
        for b in range(NB):
            movers(t, b)
            yield
        if t == 0:
            lists(1)
        else:
            tt(T.dd[:], T.zz[:], T.ownp[:], A.subtract, ["zz%d%d" % x for x in tb] + ["ownp"], ["dd"])
        yield
        if t == 0:
            act(T.junk[0:32, 0:256], T.Wl[0:32, :], F.Identity, ["Wl"], ["junk0", "acc7"], scale=-15.0, accum_out=T.acc[0:32, 7:8])
        else:
            new_parts()
        yield

    for t in range(2):
        w = 256 if t else 512
        for j in range(NV // w):
            b = j % 8
            mm(bank(b, 0, w), T.LZ[:], T.G[:, PAD + w * j:PAD + w * j + w], LZk + ["G%d" % (w * j // 1024)], b)
            out = T.Z[:, w * j:w * j + w]
            keys = ["#%d" % b] + Zk[w * j // 256:w * (j + 1) // 256]
            if t == 0 and j == 9:
                lists(0)
            if j % 2:
                ts(out, bank(b, 0, w), 0.0, A.max, [], keys)
            else:
                act(out, bank(b, 0, w), F.Relu, [], keys)
        own_keys(t)
        left = [4 * len(b[0]) for b in BATCH]
        steps = {"v": gathers(t, "V", PIECES["V"], left), "s": gathers(t, "S", PIECES["S"], left), "x": fillers(t)}
        for b in range(NB):
            steps["ABC"[b]], steps["abc"[b]] = front(t, b), back(t, b)
        for ch in ORDER:
            next(steps[ch])
        for ch in steps:
            assert next(steps[ch], 1) == 1, ch

    e0 = PAD
    for r, n in enumerate(CUT):
        b = 2 + r
        for x in range(n):
            mm(bank(b, 16 * x, 16 * x + 16), T.G[:, e0:e0 + 128], T.LC[:], Gk + ["LC"], b)
            e0 += 128
        act(T.junk[:, 256 * r:256 * r + 16 * n], bank(b, 0, 16 * n), F.Relu, [], ["#%d" % b, "junk%d" % r, "acc%d" % r],
            accum_out=T.acc[:, r:r + 1])
    pcut = T.ps[0:1, 0:8]
    mm(pcut, T.onesf[:, 0:1], T.acc[:], ["onesf"] + acck, 0)
    op("V", [], ["#0", "cb"], lambda: V.tensor_reduce(T.cb[0:1, 0:1], pcut, AxisListType.X, A.add, negate=True))
    exchange(lambda q: T.SN[q], T.LN[me], "arrN", ["SN0"], "LN")
    send([(far, T.cb[:, 0:1], far_eng), (near, T.cb[:, 0:1], [near_eng[0], near_eng[-1]])], T.CU[:, me:me + 1], "arrU", ["cb"], "LU")

    outs = [("Y", T.newpart[me:me + 1, :], T.SN[me], ["SN0"], ["o0"])]
    if me > 0:
        outs.append(("Y", T.newpart[0:me, :], T.LN[0:me], ["LN"], ["o1"]))
    if me < N - 1:
        outs.append(("Y", T.newpart[me + 1:N, :], T.LN[me + 1:N], ["LN"], ["o2"]))
    dmas("outN", outs)
    dmas("outU", [("S", T.cut[me:me + 1, :], T.cb[0:1, 0:1], ["cb"], ["u"])]
         + [(e, T.cut[lo:hi, :], T.CU[0:1, lo:hi], ["LU"], ["u" + e]) for e, lo, hi in (("Y", 0, me), ("S", me + 1, N)) if lo < hi])
    for s in total:
        g.wait_ge(T.sem[s], total[s])
